import numpy as np, ml_dtypes
CORES = [66,74,82,90,194,202,210,218]
N = 8
import mx_ref
BF = ml_dtypes.bfloat16
def gcols(t, e):
    v = np.concatenate([t.reshape(8, 16, -1, 4), np.zeros((8, 16, 1, 4), BF)], axis=2)
    return np.ascontiguousarray(np.stack([v[g][:, e[g]] for g in range(8)])).reshape(128, -1)
def tile(rs):
    return np.stack(rs, axis=2).reshape(128, -1).astype(BF)
def cut(t, i, w=512):
    return t[:, w * i:w * i + w]
def pick(q, e):
    c = np.concatenate([q[0].reshape(128, -1, 4), np.zeros((128, 1, 4), np.uint8)], axis=1); s = np.concatenate([q[1], np.ones((16, 1), np.uint8)], axis=1)
    return (np.ascontiguousarray(c[:, e].reshape(128, -1)), np.ascontiguousarray(s[:, e]))
def join(*qs):
    return (np.concatenate([q[0] for q in qs], axis=1), np.concatenate([q[1] for q in qs], axis=1))
def put(q, e, v):
    c, s = q[0].reshape(128, -1, 4).copy(), q[1].copy(); c[:, e] = v[0].reshape(128, -1, 4); s[:, e] = v[1]
    return (c.reshape(128, -1), s)
def pk(c, s):
    return (np.ascontiguousarray(c), mx_ref.live(s))
def emit(q):
    return q[0], q[1]
def packed(v, rng):
    q = [mx_ref.quantize(np.ascontiguousarray(v[r])) for r in range(N)]
    return np.stack([a for a, b in q]), np.stack([mx_ref.plane(b, rng) for a, b in q])
def values_of_codes():
    e, c = np.zeros((128, 128, 4), np.float32), np.zeros((128, 2, 4), np.uint8)
    e[np.arange(128), np.arange(128), 0] = 1
    c[:127, :, 0] = np.arange(256).reshape(2, 128).T[:127]
    return mx_ref.matmul(mx_ref.quantize(e.reshape(128, 512).astype(BF)), (c.reshape(128, 8), np.full((16, 2), 127, np.uint8))).T.reshape(-1).astype(np.float64)
CODE_VALUE, SCALE_VALUE = values_of_codes(), 2.0 ** (np.arange(256) - 127.0)
def decode(q):
    return (CODE_VALUE[q[0]].reshape(16, 8, -1, 4) * SCALE_VALUE[q[1]][:, None, :, None] + 0.0).reshape(128, -1).astype(np.float32)
def f(rng, *shape):
    return mx_ref.flush((rng.standard_normal(shape, dtype=np.float32) * np.exp2(rng.integers(-2, 3, shape[:-1] + (1,)))).astype(BF))
def wide(rng, *shape, cols=0):
    v = rng.standard_normal(shape, dtype=np.float32) * np.exp2(rng.integers(-12, 13, shape)).astype(np.float32)
    if cols: v *= np.repeat(np.exp2(rng.integers(-cols, cols + 1, shape[:-2] + (1, shape[-1] // 4))) * (rng.random(shape[:-2] + (1, shape[-1] // 4)) > 0.0625), 4, axis=-1).astype(np.float32)
    return mx_ref.flush(v.astype(BF))
C, L1, H1, L2, H2, K, R = 288, 112, 176, 64, 96, 112, 3
def big(v):
    v = v.astype(np.float32)
    v[np.abs(v) < np.float32(2.0 ** -16)] = 0
    return v.astype(BF)
def numbers_of(rng):
    return {"x": big(f(rng, N, 128, 4 * C)), "u": np.array(f(rng, N, 128, 512)), "v": np.array(f(rng, N, 128, 512))}
def layers(rng):
    return big(f(rng, N, 128, 2048)).reshape(N, 8, 16, 4, 8, 16, 4)
def weights(rng, w):
    c, p = packed(np.ascontiguousarray(w).reshape(N, 128, 2048), rng)
    return {"wc": c, "ws": p}
def setup_inputs(rng):
    return {**numbers_of(rng), **weights(rng, layers(rng))}
def setup_inputs_ties(rng):
    d = numbers_of(rng)
    x = d["x"].reshape(N, 8, 16, C, 4)
    x[:, :, 0] = 0
    x[:, :, 0, :, :2] = np.where(rng.random((N, 8, C, 2)) < 0.125, 3, rng.integers(1, 3, (N, 8, C, 2))).astype(np.float32).astype(BF)
    u = d["u"].reshape(N, 128, 128, 4)
    u[:, :, ::16] = 0
    u[:, :, 1::16] = 0
    e = int(rng.integers(N))
    k = rng.permutation(N - 2) % 2 * 2.0 - 1.0
    for i in range(N - 2):
        r = (e + 1 + i) % N
        for h in range(0, 128, 16):
            u[r, h, h, 0] = k[i]
            u[r, h, h + 1, 1] = k[i]
    w = layers(rng)
    w[:, :, :, :, :, 0] = 0
    return {"x": x.reshape(N, 128, 4 * C), "u": u.reshape(N, 128, 512), "v": d["v"], **weights(rng, w)}
def setup_inputs_near(rng):
    d = numbers_of(rng)
    x = d["x"].astype(np.float32).reshape(N, 8, 16, C, 4)
    x[:, :, 0] = 0
    x[:, :, 8:] = 0
    u = d["u"].reshape(N, 128, 128, 4)
    u[:, :, ::16] = 0
    u[:, :, 1::16] = 0
    o = rng.permutation(N) % 4
    for r in range(N):
        k = 1.0 if o[r] == 0 else 2.0 ** -30
        if o[r] < 3:
            s = rng.integers(0, 16, (8, C))
            x[r, :, 8] = ((s[:, :, None] >> np.arange(4)) & 1) * np.exp2(np.arange(4) - 23.0)
        if o[r] < 2:
            x[r, :, 0, :, 0] = 1.0 - 2.0 * o[r]
            x[r, :, 11, :, 0] = 2.0 ** -10
        if o[r] == 2: x[r, :, 0, :, 0] = -1.0 * (rng.random((8, C)) < 0.25)
        if o[r] == 3:
            s = rng.random((8, C)) < 0.25
            x[r, :, 10, :, 0] = np.where(s, 9.0, 0.0) * 2.0 ** -32
            x[r, :, 12, :, 0] = np.where(s, 0.0, 8.0) * 2.0 ** -32
        for h in range(0, 128, 16):
            for i in (h, h + 1):
                u[r, h, i, 0] = 1.0 if o[r] == 2 else k
                u[r, h + 8, i] = k
                u[r, h + 10, i, 0] = k * 1.125
                u[r, h + 11, i, 0] = k
                u[r, h + 12, i, 0] = k * 1.25
    w = layers(rng)
    w[:, :, :, :, :, 0] = 0
    w[:, :, :, :, :, 8:] = 0
    return {"x": x.reshape(N, 128, 4 * C).astype(BF), "u": u.reshape(N, 128, 512), "v": d["v"], **weights(rng, w)}
def setup_inputs_huge(rng):
    d = numbers_of(rng)
    e = rng.permutation(N)
    x = -0.6 - 0.4 * rng.random((N, 8, 16, C, 4))
    a = 0.9 + 0.1 * rng.random((N, 128, 128, 4))
    x[e[0], :, :15] = -1.0
    for i in (L1 - 1, H1 + 1): x[e[0], :, :, i] = -0.625
    a[e[0]] = 1.0
    u = d["u"].astype(np.float32).reshape(N, 128, 128, 4)
    for r in range(N):
        both = r in e[1::2]
        if both: x[r] *= rng.choice([-1.0, 1.0], (8, 1, C, 1))
        for h in range(0, 128, 16):
            i = slice(h, h + 16) if both else slice(0, 128)
            u[r, :, h:h + 2] = 0
            u[r, i, h:h + 2] = 2.0 ** 30 * a[r, i, h:h + 2]
    w = np.zeros((N, 128, 4, 128, 4), np.float32)
    i = np.arange(128)
    for b in range(4): w[:, i, b, i, b] = -1
    return {"x": (2.0 ** 30 * x).astype(np.float32).reshape(N, 128, 4 * C).astype(BF), "u": u.astype(BF).reshape(N, 128, 512), "v": d["v"], **weights(rng, w.astype(BF))}
def setup_inputs_edge(rng):
    d = numbers_of(rng)
    x = d["x"].reshape(N, 8, 16, C, 4)
    c = np.where(rng.random((N, 8)) < 0.25, rng.integers(L1, H1 + 1, (N, 8)), rng.choice([L1, H1], (N, 8)))
    k = np.where(rng.random((N, 8)) < 0.25, rng.integers(L2, H2 + 1, (N, 8)), rng.choice([L2, H2], (N, 8)))
    e = int(rng.integers(N))
    for r in (e, (e + 1) % N):
        c[r] = H1
        k[r] = L2
    x[:, :, 0] = 0
    x[:, :, 0, :, :2] = rng.integers(-1, 2, (N, 8, C, 2)).astype(np.float32).astype(BF)
    for i in (L1 - 1, H1 + 1): x[:, :, 0, i, 0] = 4.0
    for i in (L2 - 1, H2 + 1): x[:, :, 0, i, 1] = 4.0
    for r in range(N):
        for g in range(8):
            x[r, g, 0, c[r, g], 0] = 2.0
            x[r, g, 0, k[r, g], 1] = 2.0
    n = (N, 8, 8, C, 4)
    s = np.exp2(-1.0 * rng.integers(8, 15, n)) * (1.0 + (2 * rng.integers(0, 64, n) + 1) * 2.0 ** -7) * rng.choice([-1.0, 1.0], n)
    s[:, :, 0, :, 0] = 1.96875 * rng.choice([-1.0, 1.0], (N, 8, C))
    x[:, :, 8:] = s.astype(np.float32).astype(BF)
    u = d["u"].reshape(N, 128, 128, 4)
    u[:, :, ::16] = 0
    u[:, :, 1::16] = 0
    for h in range(0, 128, 16):
        u[:, h, h, 0] = 1
        u[:, h, h + 1, 1] = 1
    return {"x": x.reshape(N, 128, 4 * C), "u": u.reshape(N, 128, 512), "v": d["v"], **weights(rng, layers(rng))}
def setup_inputs_spread(rng):
    d = setup_inputs(rng)
    d["x"] = big(wide(rng, N, 128, 4 * C, cols=6))
    return d
def check_inputs(d):
    b = []
    for k in ("x", "u", "v"):
        a = np.abs(d[k].astype(np.float32))
        if not (np.isfinite(a).all() and ((a == 0) | (a >= 2.0 ** -30) & (a <= 2.0 ** 30)).all()): b.append("a value of " + k)
    none, least, most = [emit(mx_ref.quantize(np.full((128, 16), k, np.float32).astype(BF)))[1][0, 0] for k in (0.0, 2.0 ** -30, 2.0 ** 30)]
    for r in range(N):
        if ((d["wc"][r] == 0x7F) | (d["wc"][r] == 0xFF)).any(): b.append("wc: a code that is no number")
        s = mx_ref.live(d["ws"][r])
        if ((s != none) & ((s < least) | (s > most))).any(): b.append("ws: a scale out of range")
    return b
def folded(c, k):
    p = np.arange(C)
    q = np.where(p < c, c - 1 - p, p - c)
    z = np.where(q < k, k - 1 - q, q - k)
    right = (p >= c).astype(np.int64)
    leaf = np.where(q < k, right, 3 - right)
    o = np.argsort(4 * z + leaf, axis=1)
    zo = np.take_along_axis(z, o, axis=1)
    first = np.ones((8, C), bool)
    first[:, 1:] = zo[:, 1:] != zo[:, :-1]
    low, above = np.full((8, K), -1), C + z
    g, j = np.nonzero(first)
    low[g, zo[g, j]] = o[g, j]
    g, j = np.nonzero(~first)
    above[g, o[g, j - 1]] = o[g, j]
    return o, low, above
def reference(x, u, v, wc, ws):
    qu = [mx_ref.quantize(u[r]) for r in range(N)]
    lay = [pk(wc[r], ws[r]) for r in range(N)]
    now = [x[r] for r in range(N)]
    for t in range(R):
        own, folds, sent = [], [], []
        for r in range(N):
            q = mx_ref.quantize(now[r])
            own.append(decode(q))
            s = mx_ref.matmul(qu[r], q) + np.float32(0.0)
            c = L1 + np.argmax(s[::16, L1:H1 + 1], axis=1)
            k = L2 + np.argmax(s[1::16, L2:H2 + 1], axis=1)
            folds.append(folded(c[:, None], k[:, None]))
            sent.append(mx_ref.quantize(gcols(now[r], folds[r][1])))
        came = decode(join(*sent)).astype(BF)
        for r in range(N):
            o, low, above = folds[r]
            a = np.concatenate([own[r].astype(BF), cut(came, (r + 1) % N, 4 * K)], axis=1)
            z = mx_ref.quantize(((own[r] + gcols(a, above).astype(np.float32)) * np.float32(0.5)).astype(BF))
            made = tile([mx_ref.matmul(pick(lay[r], np.arange(128 * b, 128 * b + 128)), z) * np.float32(0.03125) + own[r][:, b::4] for b in range(4)])
            now[r] = gcols(made, o)
    y, lo = np.zeros((N, 128, C), np.float32), np.zeros((N, 8, C), np.float32)
    oc, osc = np.zeros((N, 128, 4 * C), np.uint8), np.zeros((N, 16, C), np.uint8)
    for r in range(N):
        q = mx_ref.quantize(now[r])
        y[r] = mx_ref.matmul(mx_ref.quantize(v[r]), q)
        lo[r] = folds[r][0]
        oc[r], osc[r] = emit(q)
    return {"y": y, "lo": lo, "oc": oc, "osc": osc}

@@ -1,0 +1,489 @@
+import numpy as np
+from concourse.mybir import dt, AluOpType, AxisListType, ActivationFunctionType
+
+C, K, ROUNDS = 288, 112, 3
+L1, H1, L2, H2 = 112, 176, 64, 96
+A, H = 64, 192
+MID = 136
+PAD = 16
+CUT = 144
+NE = 4 * C // 16
+NL = NE + C // 16
+NW = 12288
+
+SCAL = [("nc4", -4.0, 0.0, 0.0), ("nmid4", -4.0, -2.0, 0.0), ("n2", -1.0, -1.0, 288.0), ("k", 0.0, 1.0, 0.0), ("nk4", 0.0, -4.0, 0.0),
+        ("m8k", 0.0, -8.0, 0.0), ("k8", 0.0, 8.0, 0.0), ("kh4", 0.0, 2.0, 0.0), ("k2", 0.0, 2.0, 0.0), ("h2", 0.0, -2.0, 288.24),
+        ("n3", 1.0, -1.0, 0.0), ("n34", 4.0, -4.0, 0.0), ("c4", 4.0, 0.0, -2.0), ("c8", 8.0, 0.0, -4.0)]
+NS = 16
+
+F32, BF, I32, U16, U8, X4 = "float32", "bfloat16", "int32", "uint16", "uint8", "float8_e4m3fn_x4"
+SCRATCH = {
+    "X": ("sbuf", [128, PAD + 4 * C], BF), "Bt": ("sbuf", [128, 512], BF), "Z": ("sbuf", [128, 4 * C], BF),
+    "Y": ("sbuf", [128, 4 * C], BF), "FG": ("sbuf", [128, 4 * (C + K)], BF), "AN": ("sbuf", [128, 4 * (C - CUT)], BF),
+    "FO": ("sbuf", [128, 4 * CUT], BF), "FB": ("sbuf", [128, 4 * (C - CUT)], BF),
+    "ut": ("sbuf", [128, 512], BF), "vt": ("sbuf", [128, 512], BF),
+    "QU": ("sbuf", [128, 128], X4), "SU": ("sbuf", [128, 128], U8), "QUU": ("sbuf", [128, 256], X4), "SUU": ("sbuf", [128, 256], U8),
+    "QV": ("sbuf", [128, 128], X4), "SV": ("sbuf", [128, 128], U8),
+    "WQ": ("sbuf", [128, 512], X4), "WS": ("sbuf", [128, 512], U8),
+    "QS": ("sbuf", [128, 128], X4), "SS": ("sbuf", [128, 128], U8),
+    "QZ": ("sbuf", [128, C], X4), "SZ": ("sbuf", [128, C], U8),
+    "QL": ("sbuf", [128, C], X4), "SL": ("sbuf", [128, C], U8),
+    "EH": ("sbuf", [128, 528], BF), "EB": ("sbuf", [128, 528], BF), "KI": ("sbuf", [128, 528], F32),
+    "QEH": ("sbuf", [128, 512], X4), "SEH": ("sbuf", [128, 512], U8), "QEB": ("sbuf", [128, 512], X4), "SEB": ("sbuf", [128, 512], U8),
+    "m16": ("sbuf", [128, NE], I32), "pi": ("sbuf", [128, 1], I32), "pa": ("sbuf", [128, 1], I32), "pf": ("sbuf", [128, 1], F32),
+    "ei": ("sbuf", [128, NE], I32), "ji": ("sbuf", [128, NE], I32), "ti": ("sbuf", [128, NE], I32),
+    "J": ("sbuf", [128, NL], F32), "J4": ("sbuf", [128, NL], F32), "TT": ("sbuf", [128, NL], F32),
+    "EF": ("sbuf", [128, NE], F32), "S4": ("sbuf", [128, NE], F32), "AM": ("sbuf", [128, NE], F32), "TM": ("sbuf", [128, NE], F32),
+    "EQ": ("sbuf", [128, 12], F32), "ET0": ("sbuf", [128, 28], F32), "ET2": ("sbuf", [128, 12], F32), "ET3": ("sbuf", [128, 12], F32),
+    "low": ("sbuf", [128, 72], F32),
+    "ulist": ("sbuf", [128, 16], I32), "uoff": ("sbuf", [128, 16], U16),
+    "CC": ("sbuf", [128, NS], F32), "CK": ("sbuf", [128, NS], F32), "C0": ("sbuf", [128, NS], F32),
+    "CJ": ("sbuf", [128, 4 * C], F32), "LO": ("sbuf", [128, C], F32), "yt": ("sbuf", [128, C], F32),
+    "WK": ("sbuf", [128, NW], F32),
+}
+for _i in range(8):
+    SCRATCH["P%d" % _i] = ("psum", [128, 512], F32)
+for _i in range(ROUNDS):
+    SCRATCH["QX%d" % _i] = ("sbuf", [128, C + K], X4)
+    SCRATCH["SX%d" % _i] = ("sbuf", [128, C + K], U8)
+    SCRATCH["QB%d" % _i] = ("sbuf", [128, 128], X4)
+    SCRATCH["SB%d" % _i] = ("sbuf", [128, 128], U8)
+    SCRATCH["lb%d" % _i] = ("sbuf", [128, 28], U16)
+    SCRATCH["la%d" % _i] = ("sbuf", [128, NE], U16)
+    SCRATCH["lx%d" % _i] = ("sbuf", [128, NL + 2], U16)
+    SCRATCH["oi%d" % _i] = ("sbuf", [128, NL], I32)
+DMAS = ["d%d" % i for i in range(24)]
+SEMAPHORES = ["ev", "ea", "et", "eg"] + DMAS + ["gone"] + ["came%d" % i for i in range(ROUNDS)]
+BACK = 240.0
+EXCHANGE, LOAD = 3000.0, 2200.0
+plan = {}
+
+
+def planner(g, T):
+    queue = {"v": g.vector, "a": g.scalar, "t": g.tensor, "g": g, "sy": g.sync}
+    sem_of = {"v": "ev", "a": "ea", "t": "et", "g": "eg"}
+    nodes, log = [], {}
+
+    def hits(x, y):
+        return x[1] < y[2] and y[1] < x[2] and (x[3] is None or y[3] is None or x[3] == y[3])
+
+    def op(q, call, reads, writes, cost, kind="op", acc=False, after=None, late=0.0):
+        reads = [r if len(r) == 4 else r + (None,) for r in reads]
+        writes = [r if len(r) == 4 else r + (None,) for r in writes]
+        deps, soft = set(), set()
+        for regs, wr in ((reads, False), (writes, True)):
+            for r in regs:
+                for (o, reg, w) in log.get(r[0], []):
+                    if (wr or w) and hits(r, reg):
+                        (soft if acc and nodes[o]["q"] == "t" and w and wr else deps).add(o)
+        if after is not None:
+            soft.add(after)
+        i = len(nodes)
+        nodes.append({"q": q, "call": call, "deps": deps, "soft": soft - deps, "cost": cost, "kind": kind, "late": late})
+        for r in writes:
+            log[r[0]] = [e for e in log.get(r[0], []) if acc or not (r[1] <= e[1][1] and e[1][2] <= r[2] and (r[3] is None or r[3] == e[1][3]))]
+            log[r[0]].append((i, r, True))
+        for r in reads:
+            log.setdefault(r[0], []).append((i, r, False))
+        return i
+
+    def order():
+        n = len(nodes)
+        if n in plan:
+            return plan[n]
+        pre = [[(p, BACK + nodes[p]["late"]) for p in sorted(d["deps"])] + [(p, nodes[p]["late"]) for p in sorted(d["soft"])] for d in nodes]
+        cost = [d["cost"] for d in nodes]
+        prio = [c + d["late"] for c, d in zip(cost, nodes)]
+        for i in range(n - 1, -1, -1):
+            for p, b in pre[i]:
+                prio[p] = max(prio[p], cost[p] + b + prio[i])
+        left = [len(x) for x in pre]
+        out = [[] for _ in nodes]
+        for i in range(n):
+            for p, b in pre[i]:
+                out[p].append(i)
+        free = {q: 0.0 for q in queue}
+        todo = {q: [i for i in range(n) if nodes[i]["q"] == q] for q in queue}
+        est, end, seq = [0.0] * n, [None] * n, []
+        while len(seq) < n:
+            for i in range(n):
+                if end[i] is None:
+                    e = free[nodes[i]["q"]]
+                    for p, b in pre[i]:
+                        x = (est[p] + cost[p] if end[p] is None else end[p]) + b
+                        if x > e:
+                            e = x
+                    est[i] = e
+            best = spare = None
+            for q in queue:
+                can = [i for i in todo[q] if not left[i]]
+                if not can:
+                    continue
+                s = min(est[i] for i in can)
+                pick = max((i for i in can if est[i] <= s + 1.0), key=lambda i: prio[i])
+                if spare is None or est[pick] < est[spare]:
+                    spare = pick
+                for i in sorted(can, key=lambda i: est[i] - 0.001 * prio[i]):
+                    hold = False
+                    for m in todo[q]:
+                        if m != i and prio[m] > prio[i] and est[m] < est[i] + cost[i]:
+                            if max(est[i] + prio[i], est[i] + cost[i] + prio[m]) > max(est[m] + prio[m], est[m] + cost[m] + prio[i]):
+                                hold = True
+                                break
+                    if not hold:
+                        if best is None or est[i] < est[best]:
+                            best = i
+                        break
+            pick = spare if best is None else best
+            end[pick] = est[pick] + cost[pick]
+            free[nodes[pick]["q"]] = end[pick]
+            todo[nodes[pick]["q"]].remove(pick)
+            seq.append(pick)
+            for j in out[pick]:
+                left[j] -= 1
+        plan[n] = seq
+        return seq
+
+    def emit():
+        count, free = {}, list(DMAS)
+        known = {q: {} for q in queue}
+
+        def need(q, s, n, more):
+            if known[q].get(s, 0) < n:
+                queue[q].wait_ge(T.sem[s], int(n))
+                known[q][s] = n
+            for s2, n2 in more.items():
+                if known[q].get(s2, 0) < n2:
+                    known[q][s2] = n2
+        for k, i in enumerate(order()):
+            d = nodes[i]
+            q, top = d["q"], {}
+            for p in d["deps"]:
+                o = nodes[p]
+                if "s" in o and (o["s"] not in top or top[o["s"]]["n"] < o["n"]):
+                    top[o["s"]] = o
+            for o in sorted(top.values(), key=lambda o: -o["at"]):
+                need(q, o["s"], o["n"], o["k"])
+            ins = d["call"]()
+            if d["kind"] in ("op", "dma"):
+                if d["kind"] == "dma":
+                    s, n, up = free.pop(0), 16, 16
+                else:
+                    s, up = sem_of[q], 1
+                    n = count.get(s, 0) + 1
+                ins.then_inc(T.sem[s], up)
+                count[s] = n
+                d["s"], d["n"], d["k"], d["at"] = s, n, dict(known[q]), k
+        for s, n in count.items():
+            need("g", s, n, {})
+    return op, emit
+
+
+def rank_program(g, core, T, topo):
+    rank = T.rank_of(core)
+    if rank is None:
+        return
+    op, emit = planner(g, T)
+    M = AluOpType
+    AF = ActivationFunctionType
+    ts_, tt_ = g.vector.tensor_scalar, g.vector.tensor_tensor
+    to, frm = T.cores[(rank - 1) % len(T.cores)], T.cores[(rank + 1) % len(T.cores)]
+    CY = 0.83
+
+    def ap(r):
+        t = T[r[0]]
+        return t[:, r[1] + r[3]:r[2]:4] if len(r) == 4 else t[:, r[1]:r[2]]
+
+    def wide(r):
+        return (r[2] - r[1]) // (4 if len(r) == 4 else 1)
+
+    def cols(s):
+        return [x for x in s if not isinstance(x, (int, float))]
+
+    def val(s):
+        return s if isinstance(s, (int, float)) else ap(s)
+
+    used = [0]
+
+    def new(n):
+        n0 = used[0]
+        used[0] = n0 + n + n % 4
+        return ("WK", n0, n0 + n)
+
+    def ts(out, in0, s1, op0, s2=None, op1=None):
+        out = out or new(wide(in0))
+        if op1 is None:
+            op("v", lambda: ts_(ap(out), ap(in0), val(s1), None, op0), [in0] + cols([s1]), [out], CY * max(64, wide(in0)))
+        else:
+            op("v", lambda: ts_(ap(out), ap(in0), val(s1), val(s2), op0, op1), [in0] + cols([s1, s2]), [out], CY * max(64, wide(in0)))
+        return out
+
+    def tt(out, in0, in1, o):
+        out = out or new(wide(in0))
+        op("v", lambda: tt_(ap(out), ap(in0), ap(in1), o), [in0, in1], [out], CY * max(64, wide(in0) * (1 if in0[0][0] == "P" else 2)))
+        return out
+
+    def cp(out, in0):
+        op("v", lambda: g.vector.tensor_copy(ap(out), ap(in0)), [in0], [out], CY * max(64, wide(in0)))
+
+    def fill(out, x):
+        op("v", lambda: g.vector.memset(ap(out), x), [], [out], CY * max(64, wide(out)))
+
+    def act(out, in0, func, bias=0.0, scale=1.0):
+        out = out or new(wide(in0))
+        op("a", lambda: g.scalar.activation(ap(out), ap(in0), func, bias=val(bias), scale=val(scale)), [in0] + cols([bias, scale]), [out],
+           20 + CY * max(64, wide(in0)))
+        return out
+
+    def gather(q, out, win, off, scale=None):
+        cost = 60 + 1.5 * CY * wide(out)
+        if scale is not None and q == "v":
+            op("v", lambda: ts_(ap(out), ap(win).indirect(ap(off)), scale, None, M.mult), [win, off], [out], cost)
+        elif scale is not None:
+            op("a", lambda: g.scalar.activation(ap(out), ap(win).indirect(ap(off)), AF.Copy, scale=scale), [win, off], [out], cost)
+        elif q == "v":
+            op("v", lambda: g.vector.tensor_copy(ap(out), ap(win).indirect(ap(off))), [win, off], [out], cost)
+        else:
+            op("a", lambda: g.scalar.activation(ap(out), ap(win).indirect(ap(off)), AF.Copy), [win, off], [out], cost)
+
+    def quant(q, s, lo, n, tile):
+        op("v", lambda: g.vector.quantize_mx(T[q][:, lo:lo + n], T[s][:, lo:lo + n], ap(tile)), [tile], [(q, lo, lo + n), (s, lo, lo + n)], 12 + 0.88 * n)
+
+    def mm(bank, n, w, ws, wl, x, xs, xl, start=True, stop=True, after=None):
+        out = ("P%d" % bank, 0, 512)
+        op("t", lambda: g.tensor.matmul_mx(T[out[0]][:, 0:n], T[w][:, wl:wl + 128], T[ws][:, wl:wl + 128], T[x][:, xl:xl + n], T[xs][:, xl:xl + n], start, stop),
+           [(w, wl, wl + 128), (ws, wl, wl + 128), (x, xl, xl + n), (xs, xl, xl + n)], [out], 0.6 * (n + 16), acc=not start, after=after)
+
+    dq = {"sy": g.sync, "a": g.scalar, "g": g}
+
+    def load(q, out, src):
+        dst = ap(out).bitcast(dt.uint8) if out[0] == "WQ" else ap(out)
+        op(q, lambda: dq[q].dma_start(dst, src), [], [out], 60.0, "dma", late=LOAD)
+
+    def store(q, dst, src, reg):
+        op(q, lambda: dq[q].dma_start(dst, src), [reg], [], 60.0, "dma", late=LOAD)
+
+    def iota(out, pattern, base, mult):
+        cost = 130 + 2 * CY * wide(out)
+        if out[0] in ("KI", "CJ"):
+            op("g", lambda: g.iota(ap(out), pattern, base, mult, allow_small_or_imprecise_dtypes=True), [], [out], cost)
+        else:
+            op("g", lambda: g.iota(ap(out), pattern, base, mult), [], [out], cost)
+
+    load("sy", ("X", PAD + 4 * A, PAD + 4 * H), T.x[:, 4 * A:4 * H])
+    load("a", ("ut", 0, 512), T.u[:, :])
+    load("sy", ("X", PAD + 4 * H, PAD + 4 * C), T.x[:, 4 * H:4 * C])
+    load("sy", ("X", PAD, PAD + 4 * A), T.x[:, 0:4 * A])
+    load("sy", ("WQ", 0, 512), T.wc[:, :])
+    load("sy", ("WS", 0, 512), T.ws[:, :])
+    load("sy", ("vt", 0, 512), T.v[:, :])
+
+    iota(("pi", 0, 1), [[1, 1]], 0, 1)
+    iota(("m16", 0, NE), [[16, NE]], 0, 0)
+    iota(("ulist", 0, 8), [[16, 8]], 0, 0)
+    iota(("ulist", 8, 16), [[16, 8]], 1, 0)
+    iota(("KI", 0, 520), [[1, 520]], -3, -4)
+    fill(("low", 0, 72), -1.0e29)
+    ts(("pa", 0, 1), ("pi", 0, 1), 15, M.bitwise_and)
+    cp(("pf", 0, 1), ("pa", 0, 1))
+    fill(("X", 0, PAD), 0.0)
+    fill(("Bt", 4 * K, 512), 0.0)
+    ts(("ei", 0, NE), ("m16", 0, NE), ("pf", 0, 1), M.add)
+    ts(("ti", 0, NE), ("ei", 0, NE), 3, M.bitwise_and)
+    ts(("ji", 0, NE), ("ei", 0, NE), 2, M.arith_shift_right)
+    cp(("TT", 0, NE), ("ti", 0, NE))
+    cp(("J", 0, NE), ("ji", 0, NE))
+    cp(("EF", 0, NE), ("ei", 0, NE))
+    ts(("EQ", 0, 12), ("ei", 16, 28), 0.25, M.mult, -64.0, M.add)
+    ts(("ET0", 0, 28), ("ei", 0, 28), 0.25, M.mult, 52.0, M.add)
+    ts(("ET2", 0, 12), ("ei", 16, 28), 0.25, M.mult, 180.0, M.add)
+    m4 = ts(None, ("J", 0, NE), -4.0, M.mult)
+    tt(("AM", 0, NE), m4, ("TT", 0, NE), M.add)
+    ts(("ET3", 0, 12), ("AM", 16, 28), 0.25, M.mult, 51.0, M.add)
+    cp(("J", NE, NL), ("ei", 0, NL - NE))
+    fill(("TT", NE, NL), 0.0)
+    for t, f in (("CK", lambda e: e[2]), ("C0", lambda e: e[3] + L1 * e[1] + L2 * e[2]), ("CC", lambda e: e[1])):
+        def put(i, j, x, t=t):
+            if t == "CK":
+                fill((t, i, j), x)
+            else:
+                act((t, i, j), ("low", i, j), AF.Identity, bias=x, scale=0.0)
+        put(0, NS, 0.0)
+        i = 0
+        while i < len(SCAL):
+            j = i
+            while j < len(SCAL) and f(SCAL[j]) == f(SCAL[i]):
+                j += 1
+            if f(SCAL[i]) != 0.0:
+                put(i, j, float(f(SCAL[i])))
+            i = j
+    act(("S4", 0, NE), ("J", 0, NE), AF.Identity, bias=2.0, scale=4.0)
+    act(("J4", 0, NL), ("J", 0, NL), AF.Copy, scale=0.25)
+    act(("TM", 0, NE), ("TT", 0, NE), AF.Identity, bias=-898.0)
+    cp(("uoff", 0, 16), ("ulist", 0, 16))
+    ts(("EH", 0, 520), ("KI", 0, 520), 0.0, M.is_equal, 0.5, M.mult)
+    act(("EB", 0, 520), ("EH", 0, 520), AF.Copy, scale=64.0)
+
+    quant("QU", "SU", 0, 128, ("ut", 0, 512))
+    op("v", lambda: g.vector.tensor_copy(T.QUU[:, 0:256].bitcast(dt.uint32), T.QU[:, 0:128].bitcast(dt.uint32).indirect(T.uoff[:, 0:16])),
+       [("QU", 0, 128), ("uoff", 0, 16)], [("QUU", 0, 256)], 380.0)
+    op("a", lambda: g.scalar.activation(T.SUU[:, 0:256], T.SU[:, 0:128].indirect(T.uoff[:, 0:16]), AF.Copy), [("SU", 0, 128), ("uoff", 0, 16)],
+       [("SUU", 0, 256)], 400.0)
+
+    for r in range(ROUNDS):
+        last = r == ROUNDS - 1
+        qx, sx, qb, sb, lb, la, lx = ["%s%d" % (s, r) for s in ("QX", "SX", "QB", "SB", "lb", "la", "lx")]
+        quant("QS", "SS", 0, 128, ("X", PAD + 4 * A, PAD + 4 * H))
+        mm(1, 128, "QUU", "SUU", 128, "QS", "SS", 0)
+        mm(0, 128, "QUU", "SUU", 0, "QS", "SS", 0)
+
+        def first(bank, lo, n):
+            run, m, out = new(n), new(n), new(1)
+            top = ("WK", run[2] - 1, run[2])
+            op("v", lambda: g.vector.tensor_tensor_scan(ap(run), T["P%d" % bank][:, lo:lo + n], T.low[:, 0:n], -1.0e29, M.max, M.max),
+               [("P%d" % bank, 0, 512), ("low", 0, 72)], [run], CY * max(64, n))
+            op("a", lambda: g.scalar.activation(ap(m), ap(run), AF.Sign, bias=ap(top), scale=-1.0, accum_out=ap(out)), [run], [m, out], 100.0)
+            return out
+        kk = first(1, L2 - A, H2 - L2 + 1)
+        cc = first(0, L1 - A, H1 - L1 + 1)
+        xs = ("X", 0, PAD + 4 * C)
+        b5 = ts(None, ("ET0", 0, 16), cc, M.add, kk, M.subtract)
+        ts((lb, 0, 16), b5, 4.0, M.mult)
+        gather("a", ("Bt", 0, 256), xs, (lb, 0, 16))
+        b0 = ts(None, ("EQ", 0, 12), kk, M.is_lt)
+        b1 = ts(None, ("EQ", 0, 12), kk, M.is_ge, C + 4.0, M.mult)
+        b2 = ts(None, ("ET0", 16, 28), cc, M.add, kk, M.subtract)
+        b3 = ts(None, ("ET2", 0, 12), cc, M.add, kk, M.add)
+        b4 = ts(None, ("ET3", 0, 12), cc, M.add, kk, M.subtract)
+        b1 = tt(None, b3, b1, M.is_lt)
+        b2 = tt(None, b2, b0, M.mult)
+        b3 = tt(None, b3, b1, M.mult)
+        b2 = tt(None, b2, b4, M.max)
+        b2 = tt(None, b2, b3, M.max)
+        ts((lb, 16, 28), b2, 4.0, M.mult)
+        gather("a", ("Bt", 352, 448), xs, (lb, 22, 28))
+        gather("v", ("Bt", 256, 352), xs, (lb, 16, 22))
+        quant(qb, sb, 0, 128, ("Bt", 0, 512))
+        rid, pid = topo.addr(to, core)
+        mask = topo.mask(core, to)
+
+        def send(qx=qx, sx=sx, qb=qb, sb=sb, r=r):
+            g.remote_dma(T[qx][:, C:C + K].bitcast(dt.uint8), T[qb][:, 0:K].bitcast(dt.uint8), T.sem["came%d" % r], T.sem.gone, pid, rid, mask)
+            g.remote_dma(T[sx][:, C:C + K], T[sb][:, 0:K], T.sem["came%d" % r], T.sem.gone, pid, rid, mask)
+        sent = op("g", send, [(qb, 0, 128), (sb, 0, 128)], [], 600.0, "send", late=EXCHANGE)
+        if r == 0:
+            for b in range(4):
+                quant("QEH", "SEH", 128 * b, 128, ("EH", 3 - b, 515 - b))
+        quant(qx, sx, 0, C, ("X", PAD, PAD + 4 * C))
+        for b in range(4):
+            mm(4 + b, C, "QEH", "SEH", 128 * b, qx, sx, 0)
+        sa1 = ts(None, ("CC", 0, NS), cc, M.mult)
+        sa2 = ts(None, ("CK", 0, NS), kk, M.mult)
+        sa3 = tt(None, sa2, ("C0", 0, NS), M.add)
+        sv = tt(None, sa1, sa3, M.add)
+        sc = {e[0]: ("WK", sv[1] + i, sv[1] + i + 1) for i, e in enumerate(SCAL)}
+        EF, S4 = ("EF", 0, NE), ("S4", 0, NE)
+        s0 = act(None, S4, AF.Abs, bias=sc["nmid4"])
+        s1 = act(None, S4, AF.Abs, bias=sc["nc4"])
+        s2 = act(None, s1, AF.Abs, bias=sc["nk4"])
+        for b in range(4):
+            act(("FG", 0, 4 * C, b), ("P%d" % (4 + b), 0, C), AF.Copy)
+            act(("FO", 0, 4 * CUT, b), ("P%d" % (4 + b), 0, CUT), AF.Copy)
+        w0 = ts(None, ("AM", 0, NE), sc["c8"], M.add)
+        w2 = ts(None, EF, sc["n34"], M.is_lt, 1152.0, M.mult)
+        alt = ts(None, EF, sc["m8k"], M.add)
+        w1 = ts(None, s0, sc["kh4"], M.is_lt, sc["k8"], M.mult)
+        zt = tt(None, s2, ("TM", 0, NE), M.add)
+        w0 = tt(None, w0, w2, M.add)
+        w0 = tt(None, w0, w1, M.add)
+        w4 = ts(None, w0, 1152.0, M.is_lt, 4096.0, M.mult)
+        w4 = tt(None, w4, alt, M.add)
+        w0 = tt(None, w0, w4, M.min)
+        w5 = ts(None, w0, 0.0, M.is_lt, 2048.0, M.mult)
+        w5 = tt(None, w5, zt, M.add)
+        w0 = tt(None, w0, w5, M.max)
+        cp((la, 0, NE), w0)
+        for b in range(4):
+            mm(b, C - CUT, "QEH", "SEH", 128 * b, qx, sx, CUT)
+            act(("FB", 0, 4 * (C - CUT), b), ("P%d" % b, 0, C - CUT), AF.Copy, scale=64.0)
+        if r == 0:
+            for b in range(4):
+                quant("QEB", "SEB", 128 * b, 128, ("EB", 3 - b, 515 - b))
+        n = NL if last else NE
+        J, zi = ("J", 0, n), ("oi%d" % r, 0, n)
+        aa = tt(None, sc["n2"], sc["n3"], M.min)
+        hh = tt(None, sc["k2"], sc["h2"], M.min)
+        p0 = ts(None, J, aa, M.subtract, 1.0 / 3.0, M.mult)
+        p1 = ts(None, J, hh, M.subtract, 0.5, M.mult)
+        p2 = ts(None, J, aa, M.subtract, sc["k2"], M.subtract)
+        p0 = tt(None, p0, ("J4", 0, n), M.max)
+        p1 = tt(None, p1, p2, M.max)
+        p0 = tt(None, p0, p1, M.max)
+        ts(zi, p0, -0.35, M.add)
+        fr = tt(None, p0, zi, M.subtract)
+        mk = ts(None, zi, sc["k"], M.is_ge, 0.55, M.mult)
+        ov = ts(None, zi, sc["n2"], M.is_ge, 0.17, M.mult)
+        z2 = ts(None, zi, 2.0, M.mult, 1.0, M.add)
+        tc = ts(None, ("TT", 0, n), sc["c4"], M.add)
+        y = tt(None, fr, mk, M.add)
+        mo = tt(None, mk, ov, M.add)
+        ta = ts(None, y, 0.45, M.is_ge, 0.5, M.subtract)
+        y2 = tt(None, fr, mo, M.add)
+        y2 = act(None, y2, AF.Abs, bias=-0.45)
+        t = tt(None, ta, z2, M.mult)
+        u = ts(None, t, sc["k"], M.add, 8.0, M.mult)
+        sg = ts(None, y2, 0.25, M.is_lt, 0.5, M.subtract)
+        f = tt(None, u, sg, M.mult)
+        f = tt(None, f, tc, M.add)
+        cp((lx, 0, n), f)
+        if last:
+            iota(("CJ", 0, 4 * C), [[1, C], [0, 4]], 0, 0)
+            quant("QV", "SV", 0, 128, ("vt", 0, 512))
+        came = op("t", lambda r=r: g.tensor.wait_ge(T.sem["came%d" % r], 2 * len(topo.engines(frm, core))), [], [], 0.0, "wait", after=sent)
+        for b in range(4):
+            mm(4 + b, 128, "QEH", "SEH", 128 * b, qx, sx, C + K - 128, after=came)
+        for b in range(4):
+            out, src = ("FG", 4 * C, 4 * (C + K), b), ("P%d" % (4 + b), 128 - K, 128)
+            if b % 2:
+                act(out, src, AF.Copy)
+            else:
+                cp(out, src)
+        for b in range(4):
+            mm(4 + b, CUT, "QEB", "SEB", 128 * b, qx, sx, 0, True, False)
+        win = ("FG", 0, 4 * (C + K))
+        gather("a", ("AN", 0, 4 * (C - CUT)), win, (la, CUT // 4, C // 4))
+        off, own, out = (la, 0, CUT // 4), ("FO", 0, 4 * CUT), ("Z", 0, 4 * CUT)
+        op("v", lambda off=off, own=own, out=out: tt_(ap(out), ap(win).indirect(ap(off)), ap(own), M.add), [win, off, own], [out], 50 + 1.5 * CY * 4 * CUT)
+        quant("QZ", "SZ", 0, CUT, out)
+        for b in range(4):
+            mm(4 + b, CUT, "WQ", "WS", 128 * b, "QZ", "SZ", 0, False, True)
+        for b in range(4):
+            tt(("Z", 4 * CUT, 4 * C, b), ("P%d" % b, 0, C - CUT), ("AN", 0, 4 * (C - CUT), b), M.add)
+        quant("QZ", "SZ", CUT, C - CUT, ("Z", 4 * CUT, 4 * C))
+        for b in range(4):
+            mm(b, C - CUT, "WQ", "WS", 128 * b, "QZ", "SZ", CUT)
+        for b in range(4):
+            act(("Y", 0, 4 * CUT, b), ("P%d" % (4 + b), 0, CUT), AF.Copy)
+        for b in range(4):
+            tt(("Y", 4 * CUT, 4 * C, b), ("P%d" % b, 0, C - CUT), ("FB", 0, 4 * (C - CUT), b), M.add)
+        y, x = ("Y", 0, 4 * C), lambda lo, hi: ("X", PAD + 4 * lo, PAD + 4 * hi)
+        if not last:
+            for q, lo, hi in (("v", A, MID), ("a", MID, H), ("a", H, C), ("a", 0, A)):
+                gather(q, x(lo, hi), y, (lx, lo // 4, hi // 4), 0.03125)
+            continue
+        cut = 144
+        for q, lo, hi in (("v", 0, cut), ("a", cut, C)):
+            gather(q, x(lo, hi), y, (lx, lo // 4, hi // 4), 0.03125)
+        for i, (lo, hi) in enumerate(((0, cut), (cut, C))):
+            quant("QL", "SL", lo, hi - lo, x(lo, hi))
+            mm(i, hi - lo, "QV", "SV", 0, "QL", "SL", lo)
+        gather("a", ("LO", 0, C), ("CJ", 0, 4 * C), (lx, NE, NL))
+        cp(("yt", 0, cut), ("P0", 0, cut))
+        cp(("yt", cut, C), ("P1", 0, C - cut))
+        store("sy", T.oc[:, :], T.QL[:, 0:C].bitcast(dt.uint8), ("QL", 0, C))
+        for k in range(4):
+            store("a", T.osc[4 * k:4 * k + 4, 0:C], T.SL[32 * k:32 * k + 4, 0:C], ("SL", 0, C))
+        store("sy", T.y[:, :], T.yt[:, 0:C], ("yt", 0, C))
+        store("a", T.lo[:, :], T.LO[0:128:16, :], ("LO", 0, C))
+    emit()
+    g.wait_ge(T.sem.gone, 2 * ROUNDS * len(topo.engines(core, to)))

@@ -1,26 +1,31 @@
-import numpy as np
+import math
 from concourse.mybir import dt, AluOpType, AxisListType, ActivationFunctionType
 
 C, K, ROUNDS = 288, 112, 3
 L1, H1, L2, H2 = 112, 176, 64, 96
 A, H = 64, 192
-MID = 136
 PAD = 16
 CUT = 144
-NE = 4 * C // 16
-NL = NE + C // 16
-NW = 12288
+NC = C // 16
+NP = CUT // 16 + CUT // 16 % 2
+NA = NP + (C - CUT) // 16
+NJ = NC + A // 16
+FW = C + K
+NW = 4096
+BIG = 65536.0
+WHOLE = 12582912.0
 
-SCAL = [("nc4", -4.0, 0.0, 0.0), ("nmid4", -4.0, -2.0, 0.0), ("n2", -1.0, -1.0, 288.0), ("k", 0.0, 1.0, 0.0), ("nk4", 0.0, -4.0, 0.0),
-        ("m8k", 0.0, -8.0, 0.0), ("k8", 0.0, 8.0, 0.0), ("kh4", 0.0, 2.0, 0.0), ("k2", 0.0, 2.0, 0.0), ("h2", 0.0, -2.0, 288.24),
-        ("n3", 1.0, -1.0, 0.0), ("n34", 4.0, -4.0, 0.0), ("c4", 4.0, 0.0, -2.0), ("c8", 8.0, 0.0, -4.0)]
-NS = 16
+SCAL = [("fb", 2048.0, -2048.0, -1024.0), ("c2", 2.0, 0.0, -288.5), ("cm", 1.0, 0.0, -0.5), ("s", 1.0, 1.0, -0.5), ("n2h", -1.0, -1.0, 287.5),
+        ("k2", 0.0, 2.0, 0.0), ("nalt", 0.0, -2.0, -287.5), ("kh", 0.0, 1.0, -0.5),
+        ("a1", 1.0 / 3.0, 1.0 / 3.0, -96.0), ("nk", 0.0, -1.0, 0.0), ("c1", 1.0, -1.0, -288.0),
+        ("a2", -1.0 / 3.0, 1.0 / 3.0, 0.0), ("b2", 0.0, 1.0, -144.12), ("c3", -1.0, -1.0, 0.0)]
+NS = len(SCAL)
 
 F32, BF, I32, U16, U8, X4 = "float32", "bfloat16", "int32", "uint16", "uint8", "float8_e4m3fn_x4"
 SCRATCH = {
-    "X": ("sbuf", [128, PAD + 4 * C], BF), "Bt": ("sbuf", [128, 512], BF), "Z": ("sbuf", [128, 4 * C], BF),
-    "Y": ("sbuf", [128, 4 * C], BF), "FG": ("sbuf", [128, 4 * (C + K)], BF), "AN": ("sbuf", [128, 4 * (C - CUT)], BF),
-    "FO": ("sbuf", [128, 4 * CUT], BF), "FB": ("sbuf", [128, 4 * (C - CUT)], BF),
+    "X": ("sbuf", [128, PAD + 4 * (C + A)], BF), "Bt": ("sbuf", [128, 512], BF), "Z": ("sbuf", [128, 4 * C], BF),
+    "Y": ("sbuf", [128, 4 * C], BF), "FG": ("sbuf", [128, 4 * FW], BF), "AN": ("sbuf", [128, 4 * (C - CUT)], BF),
+    "FO": ("sbuf", [128, 4 * CUT], BF),
     "ut": ("sbuf", [128, 512], BF), "vt": ("sbuf", [128, 512], BF),
     "QU": ("sbuf", [128, 128], X4), "SU": ("sbuf", [128, 128], U8), "QUU": ("sbuf", [128, 256], X4), "SUU": ("sbuf", [128, 256], U8),
     "QV": ("sbuf", [128, 128], X4), "SV": ("sbuf", [128, 128], U8),
@@ -28,17 +33,19 @@ SCRATCH = {
     "QS": ("sbuf", [128, 128], X4), "SS": ("sbuf", [128, 128], U8),
     "QZ": ("sbuf", [128, C], X4), "SZ": ("sbuf", [128, C], U8),
     "QL": ("sbuf", [128, C], X4), "SL": ("sbuf", [128, C], U8),
-    "EH": ("sbuf", [128, 528], BF), "EB": ("sbuf", [128, 528], BF), "KI": ("sbuf", [128, 528], F32),
+    "EH": ("sbuf", [128, 528], BF), "EB": ("sbuf", [128, 528], BF), "KI": ("sbuf", [128, 128], F32),
     "QEH": ("sbuf", [128, 512], X4), "SEH": ("sbuf", [128, 512], U8), "QEB": ("sbuf", [128, 512], X4), "SEB": ("sbuf", [128, 512], U8),
-    "m16": ("sbuf", [128, NE], I32), "pi": ("sbuf", [128, 1], I32), "pa": ("sbuf", [128, 1], I32), "pf": ("sbuf", [128, 1], F32),
-    "ei": ("sbuf", [128, NE], I32), "ji": ("sbuf", [128, NE], I32), "ti": ("sbuf", [128, NE], I32),
-    "J": ("sbuf", [128, NL], F32), "J4": ("sbuf", [128, NL], F32), "TT": ("sbuf", [128, NL], F32),
-    "EF": ("sbuf", [128, NE], F32), "S4": ("sbuf", [128, NE], F32), "AM": ("sbuf", [128, NE], F32), "TM": ("sbuf", [128, NE], F32),
-    "EQ": ("sbuf", [128, 12], F32), "ET0": ("sbuf", [128, 28], F32), "ET2": ("sbuf", [128, 12], F32), "ET3": ("sbuf", [128, 12], F32),
-    "low": ("sbuf", [128, 72], F32),
+    "pi": ("sbuf", [128, 1], I32), "pa": ("sbuf", [128, 1], I32), "pf": ("sbuf", [128, 1], F32),
+    "m16": ("sbuf", [128, 28], I32), "ei": ("sbuf", [128, 28], I32), "zi": ("sbuf", [128, 12], I32),
+    "mp": ("sbuf", [128, 2 * NP], F32), "mj": ("sbuf", [128, 2 * NC], F32), "PL": ("sbuf", [128, NA], F32), "J": ("sbuf", [128, NJ], F32),
+    "PB": ("sbuf", [128, NA], F32), "J2": ("sbuf", [128, NJ], F32), "J6": ("sbuf", [128, NJ], F32),
+    "ZQ": ("sbuf", [128, 12], F32), "NZ": ("sbuf", [128, 12], F32), "ET": ("sbuf", [128, 16], F32),
+    "low": ("sbuf", [128, 96], F32),
     "ulist": ("sbuf", [128, 16], I32), "uoff": ("sbuf", [128, 16], U16),
-    "CC": ("sbuf", [128, NS], F32), "CK": ("sbuf", [128, NS], F32), "C0": ("sbuf", [128, NS], F32),
-    "CJ": ("sbuf", [128, 4 * C], F32), "LO": ("sbuf", [128, C], F32), "yt": ("sbuf", [128, C], F32),
+    "CC": ("sbuf", [128, NS], F32), "CK": ("sbuf", [128, NS], F32),
+    "PAT": ("sbuf", [128, 4 * NA], F32), "ZS": ("sbuf", [128, 336], F32), "B1": ("sbuf", [128, 36], F32), "W1": ("sbuf", [128, 4 * NA], F32),
+    "U1": ("sbuf", [128, 2 * NA], F32), "U2": ("sbuf", [128, 2 * NA], F32), "N1": ("sbuf", [128, 4 * NJ], F32),
+    "CJ": ("sbuf", [128, C], F32), "LO": ("sbuf", [128, C], F32), "yt": ("sbuf", [128, C], F32),
     "WK": ("sbuf", [128, NW], F32),
 }
 for _i in range(8):
@@ -49,13 +56,14 @@ for _i in range(ROUNDS):
     SCRATCH["QB%d" % _i] = ("sbuf", [128, 128], X4)
     SCRATCH["SB%d" % _i] = ("sbuf", [128, 128], U8)
     SCRATCH["lb%d" % _i] = ("sbuf", [128, 28], U16)
-    SCRATCH["la%d" % _i] = ("sbuf", [128, NE], U16)
-    SCRATCH["lx%d" % _i] = ("sbuf", [128, NL + 2], U16)
-    SCRATCH["oi%d" % _i] = ("sbuf", [128, NL], I32)
+    SCRATCH["la%d" % _i] = ("sbuf", [128, NA + 1], U16)
+    SCRATCH["lx%d" % _i] = ("sbuf", [128, NC], U16)
 DMAS = ["d%d" % i for i in range(24)]
 SEMAPHORES = ["ev", "ea", "et", "eg"] + DMAS + ["gone"] + ["came%d" % i for i in range(ROUNDS)]
-BACK = 240.0
-EXCHANGE, LOAD = 3000.0, 2200.0
+BACK = 180.0
+EXCHANGE, LOAD = 1800.0, 1900.0
+FIGURES = [(140.0, 1400.0, 1800.0, 1.0), (200.0, 2200.0, 2000.0, 1.0), (170.0, 1800.0, 1900.0, 1.3)]
+TRIES, SLACK, SEED, EARLY = 40000, 100.0, 12345, 0.5
 plan = {}
 
 
@@ -64,24 +72,35 @@ def planner(g, T):
     sem_of = {"v": "ev", "a": "ea", "t": "et", "g": "eg"}
     nodes, log = [], {}
 
-    def hits(x, y):
-        return x[1] < y[2] and y[1] < x[2] and (x[3] is None or y[3] is None or x[3] == y[3])
+    def bank(r):
+        return SCRATCH[r[0]][0] == "psum"
 
-    def op(q, call, reads, writes, cost, kind="op", acc=False, after=None, late=0.0):
-        reads = [r if len(r) == 4 else r + (None,) for r in reads]
-        writes = [r if len(r) == 4 else r + (None,) for r in writes]
+    def norm(r):
+        if bank(r):
+            return (r[0], 0, 512, 1)
+        return r if len(r) == 4 else r + (1,)
+
+    def hits(x, y):
+        return x[1] < y[2] and y[1] < x[2] and (x[1] - y[1]) % math.gcd(x[3], y[3]) == 0
+
+    def covers(x, y):
+        return x[1] <= y[1] and y[2] <= x[2] and y[3] % x[3] == 0 and (y[1] - x[1]) % x[3] == 0
+
+    def op(q, call, reads, writes, cost, kind="op", acc=False, after=None, late=0.0, other=None):
+        reads = [norm(r) for r in reads]
+        writes = [norm(r) for r in writes]
         deps, soft = set(), set()
         for regs, wr in ((reads, False), (writes, True)):
             for r in regs:
                 for (o, reg, w) in log.get(r[0], []):
-                    if (wr or w) and hits(r, reg):
+                    if (wr or w or bank(r)) and hits(r, reg):
                         (soft if acc and nodes[o]["q"] == "t" and w and wr else deps).add(o)
         if after is not None:
             soft.add(after)
         i = len(nodes)
-        nodes.append({"q": q, "call": call, "deps": deps, "soft": soft - deps, "cost": cost, "kind": kind, "late": late})
+        nodes.append({"q": q, "call": call, "deps": deps, "soft": soft - deps, "cost": cost, "kind": kind, "ways": [(q, call, cost), other], "late": late})
         for r in writes:
-            log[r[0]] = [e for e in log.get(r[0], []) if acc or not (r[1] <= e[1][1] and e[1][2] <= r[2] and (r[3] is None or r[3] == e[1][3]))]
+            log[r[0]] = [e for e in log.get(r[0], []) if acc or not covers(r, e[1])]
             log[r[0]].append((i, r, True))
         for r in reads:
             log.setdefault(r[0], []).append((i, r, False))
@@ -91,7 +110,8 @@ def planner(g, T):
         n = len(nodes)
         if n in plan:
             return plan[n]
-        pre = [[(p, BACK + nodes[p]["late"]) for p in sorted(d["deps"])] + [(p, nodes[p]["late"]) for p in sorted(d["soft"])] for d in nodes]
+        pre = [[(p, BACK + nodes[p]["late"]) for p in sorted(d["deps"])] + [(p, nodes[p]["late"] * (nodes[p]["kind"] == "send")) for p in sorted(d["soft"])]
+               for d in nodes]
         cost = [d["cost"] for d in nodes]
         prio = [c + d["late"] for c, d in zip(cost, nodes)]
         for i in range(n - 1, -1, -1):
@@ -141,8 +161,126 @@ def planner(g, T):
             seq.append(pick)
             for j in out[pick]:
                 left[j] -= 1
+        seq = polish(seq)
         plan[n] = seq
         return seq
+
+    def polish(seq):
+        n = len(nodes)
+        names = list(queue)
+        qs, way, cost = [names.index(d["q"]) for d in nodes], [0] * n, [d["cost"] for d in nodes]
+        two = [i for i in range(n) if nodes[i]["ways"][1]]
+        before = [set(d["deps"]) | set(d["soft"]) for d in nodes]
+        sets = []
+        for back, exchange, load, slow in FIGURES:
+            late = [exchange if d["kind"] == "send" else load if d["kind"] == "dma" else 0.0 for d in nodes]
+            sets.append(([[(p, back + late[p]) for p in sorted(d["deps"])] + [(p, late[p] * (nodes[p]["kind"] == "send")) for p in sorted(d["soft"])]
+                          for d in nodes],
+                         [slow if d["kind"] == "op" else 1.0 for d in nodes], [load if d["kind"] == "dma" else 0.0 for d in nodes]))
+
+        def run(s, fig):
+            pre, slow, tail = fig
+            free, last = [0.0] * len(queue), [-1] * len(queue)
+            end, why, top, at = [0.0] * n, [-1] * n, 0.0, -1
+            for i in s:
+                q = qs[i]
+                e, w = free[q], last[q]
+                for p, b in pre[i]:
+                    x = end[p] + b
+                    if x > e:
+                        e, w = x, p
+                e += cost[i] * slow[i]
+                end[i], why[i], free[q], last[q] = e, w, e, i
+                if e + tail[i] > top:
+                    top, at = e + tail[i], i
+            top += EARLY * sum(end) / n
+            pairs = []
+            while at >= 0:
+                w = why[at]
+                if w >= 0 and qs[w] == qs[at] and w not in before[at]:
+                    pairs.append((w, at))
+                at = w
+            return top, pairs
+
+        def flip(i):
+            way[i] = 1 - way[i]
+            q, _, c = nodes[i]["ways"][way[i]]
+            qs[i], cost[i] = names.index(q), c
+        seed = [SEED]
+
+        def draw(m):
+            seed[0] = (seed[0] * 1103515245 + 12345) % 2147483648
+            return (seed[0] >> 8) % m
+        now = [run(seq, f) for f in sets]
+        total = sum(t for t, _ in now)
+        best, kept = total, (seq, list(way))
+        for step in range(TRIES):
+            pairs = now[draw(len(sets))][1]
+            room = SLACK * (1.0 - step / TRIES) * draw(1000) / 1000.0 * (draw(3) == 0)
+            if draw(5) == 0:
+                near = [x for p in pairs for x in p if nodes[x]["ways"][1]]
+                i = near[draw(len(near))] if near and draw(2) else two[draw(len(two))]
+                moved = [i]
+                if draw(2):
+                    b = seq.index(i)
+                    near = [x for x in seq[max(0, b - 12):b + 12] if nodes[x]["ways"][1] and qs[x] != qs[i]]
+                    if near:
+                        moved.append(near[draw(len(near))])
+                for x in moved:
+                    flip(x)
+                then = [run(seq, f) for f in sets]
+                t = sum(x for x, _ in then)
+                if t <= total + room:
+                    now, total = then, t
+                    if t < best:
+                        best, kept = t, (seq, list(way))
+                else:
+                    for x in moved:
+                        flip(x)
+                continue
+            if pairs and draw(4):
+                j, i = pairs[draw(len(pairs))]
+                a, b = seq.index(j), seq.index(i)
+            else:
+                b = 1 + draw(n - 1)
+                i = seq[b]
+                a = b - 1
+                while a >= 0 and qs[seq[a]] != qs[i]:
+                    a -= 1
+                if a < 0:
+                    continue
+                j = seq[a]
+            for _ in range(draw(3) if draw(2) else 0):
+                a2 = a - 1
+                while a2 >= 0 and qs[seq[a2]] != qs[i]:
+                    a2 -= 1
+                if a2 >= 0:
+                    a = a2
+            part = seq[a:b + 1]
+            if draw(2):
+                need = {part[-1]}
+                for m in reversed(part[:-1]):
+                    if any(m in before[x] for x in need):
+                        need.add(m)
+                if part[0] in need:
+                    continue
+                part = [m for m in part if m in need] + [m for m in part if m not in need]
+            else:
+                need = {part[0]}
+                for m in part[1:]:
+                    if before[m] & need:
+                        need.add(m)
+                if part[-1] in need:
+                    continue
+                part = [m for m in part if m not in need] + [m for m in part if m in need]
+            other = seq[:a] + part + seq[b + 1:]
+            then = [run(other, f) for f in sets]
+            t = sum(x for x, _ in then)
+            if t <= total + room:
+                seq, now, total = other, then, t
+                if t < best:
+                    best, kept = t, (other, list(way))
+        return kept
 
     def emit():
         count, free = {}, list(DMAS)
@@ -155,8 +293,10 @@ def planner(g, T):
             for s2, n2 in more.items():
                 if known[q].get(s2, 0) < n2:
                     known[q][s2] = n2
-        for k, i in enumerate(order()):
+        seq, way = order()
+        for k, i in enumerate(seq):
             d = nodes[i]
+            d["q"], d["call"], d["cost"] = d["ways"][way[i]]
             q, top = d["q"], {}
             for p in d["deps"]:
                 o = nodes[p]
@@ -192,10 +332,16 @@ def rank_program(g, core, T, topo):
 
     def ap(r):
         t = T[r[0]]
-        return t[:, r[1] + r[3]:r[2]:4] if len(r) == 4 else t[:, r[1]:r[2]]
+        return t[:, r[1]:r[2]:r[3]] if len(r) == 4 else t[:, r[1]:r[2]]
 
     def wide(r):
-        return (r[2] - r[1]) // (4 if len(r) == 4 else 1)
+        return len(range(r[1], r[2], r[3] if len(r) == 4 else 1))
+
+    def half(*rs):
+        return 0.5 if all(SCRATCH[r[0]][2] == BF for r in rs) else 1.0
+
+    def slot(r, i, step=4):
+        return (r[0], r[1] + i, r[2], step)
 
     def cols(s):
         return [x for x in s if not isinstance(x, (int, float))]
@@ -207,7 +353,7 @@ def rank_program(g, core, T, topo):
 
     def new(n):
         n0 = used[0]
-        used[0] = n0 + n + n % 4
+        used[0] = n0 + n + (-n) % 4
         return ("WK", n0, n0 + n)
 
     def ts(out, in0, s1, op0, s2=None, op1=None):
@@ -223,11 +369,36 @@ def rank_program(g, core, T, topo):
         op("v", lambda: tt_(ap(out), ap(in0), ap(in1), o), [in0, in1], [out], CY * max(64, wide(in0) * (1 if in0[0][0] == "P" else 2)))
         return out
 
-    def cp(out, in0):
-        op("v", lambda: g.vector.tensor_copy(ap(out), ap(in0)), [in0], [out], CY * max(64, wide(in0)))
+    def scan(out, d0, d1, op0, op1, first=0.0):
+        out = out or new(wide(d0))
+        op("v", lambda: g.vector.tensor_tensor_scan(ap(out), ap(d0), ap(d1), first, op0, op1), [d0, d1], [out], CY * max(64, wide(d0)))
+        return out
 
-    def fill(out, x):
-        op("v", lambda: g.vector.memset(ap(out), x), [], [out], CY * max(64, wide(out)))
+    def either(q, reads, out, on_v, on_s):
+        ways = [("v",) + on_v, ("a",) + on_s]
+        if q == "a":
+            ways.reverse()
+        op(ways[0][0], ways[0][1], reads, [out], ways[0][2], other=ways[1])
+        return out
+
+    def cp(out, in0, q=None):
+        on_v = (lambda: g.vector.tensor_copy(ap(out), ap(in0)), CY * max(64, wide(in0) * half(out, in0)))
+        if q is None:
+            return op("v", on_v[0], [in0], [out], on_v[1])
+        either(q, [in0], out, on_v, (lambda: g.scalar.activation(ap(out), ap(in0), AF.Copy), 20 + CY * max(64, wide(in0))))
+
+    def fill(out, x, q=None):
+        on_v = (lambda: g.vector.memset(ap(out), x), CY * max(64, wide(out) * half(out)))
+        if q is None:
+            return op("v", on_v[0], [], [out], on_v[1])
+        src = ("low", 0, wide(out))
+        either(q, [src], out, on_v, (lambda: g.scalar.activation(ap(out), ap(src), AF.Identity, bias=x, scale=0.0), 20 + CY * max(64, wide(out))))
+
+    def lin(q, out, in0, scale, bias):
+        out = out or new(wide(in0))
+        return either(q, [in0] + cols([scale, bias]), out,
+                      (lambda: ts_(ap(out), ap(in0), val(scale), val(bias), M.mult, M.add), CY * max(64, wide(in0) * half(out, in0))),
+                      (lambda: g.scalar.activation(ap(out), ap(in0), AF.Identity, bias=val(bias), scale=val(scale)), 20 + CY * max(64, wide(in0))))
 
     def act(out, in0, func, bias=0.0, scale=1.0):
         out = out or new(wide(in0))
@@ -236,93 +407,107 @@ def rank_program(g, core, T, topo):
         return out
 
     def gather(q, out, win, off, scale=None):
-        cost = 60 + 1.5 * CY * wide(out)
-        if scale is not None and q == "v":
-            op("v", lambda: ts_(ap(out), ap(win).indirect(ap(off)), scale, None, M.mult), [win, off], [out], cost)
-        elif scale is not None:
-            op("a", lambda: g.scalar.activation(ap(out), ap(win).indirect(ap(off)), AF.Copy, scale=scale), [win, off], [out], cost)
-        elif q == "v":
-            op("v", lambda: g.vector.tensor_copy(ap(out), ap(win).indirect(ap(off))), [win, off], [out], cost)
+        cost = 1.5 * CY * wide(out)
+        if scale is not None:
+            either(q, [win, off], out, (lambda: ts_(ap(out), ap(win).indirect(ap(off)), scale, None, M.mult), 50 + cost),
+                   (lambda: g.scalar.activation(ap(out), ap(win).indirect(ap(off)), AF.Copy, scale=scale), 65 + cost))
         else:
-            op("a", lambda: g.scalar.activation(ap(out), ap(win).indirect(ap(off)), AF.Copy), [win, off], [out], cost)
+            either(q, [win, off], out, (lambda: g.vector.tensor_copy(ap(out), ap(win).indirect(ap(off))), 50 + cost),
+                   (lambda: g.scalar.activation(ap(out), ap(win).indirect(ap(off)), AF.Copy), 65 + cost))
 
     def quant(q, s, lo, n, tile):
         op("v", lambda: g.vector.quantize_mx(T[q][:, lo:lo + n], T[s][:, lo:lo + n], ap(tile)), [tile], [(q, lo, lo + n), (s, lo, lo + n)], 12 + 0.88 * n)
 
     def mm(bank, n, w, ws, wl, x, xs, xl, start=True, stop=True, after=None):
         out = ("P%d" % bank, 0, 512)
-        op("t", lambda: g.tensor.matmul_mx(T[out[0]][:, 0:n], T[w][:, wl:wl + 128], T[ws][:, wl:wl + 128], T[x][:, xl:xl + n], T[xs][:, xl:xl + n], start, stop),
-           [(w, wl, wl + 128), (ws, wl, wl + 128), (x, xl, xl + n), (xs, xl, xl + n)], [out], 0.6 * (n + 16), acc=not start, after=after)
+        return op("t", lambda: g.tensor.matmul_mx(T[out[0]][:, 0:n], T[w][:, wl:wl + 128], T[ws][:, wl:wl + 128], T[x][:, xl:xl + n], T[xs][:, xl:xl + n],
+                                                  start, stop),
+                  [(w, wl, wl + 128), (ws, wl, wl + 128), (x, xl, xl + n), (xs, xl, xl + n)], [out], 0.6 * (n + 16), acc=not start, after=after)
 
-    dq = {"sy": g.sync, "a": g.scalar, "g": g}
+    dq, dmas = {"sy": g.sync, "a": g.scalar, "g": g}, {}
 
     def load(q, out, src):
         dst = ap(out).bitcast(dt.uint8) if out[0] == "WQ" else ap(out)
-        op(q, lambda: dq[q].dma_start(dst, src), [], [out], 60.0, "dma", late=LOAD)
+        dmas[q] = op(q, lambda: dq[q].dma_start(dst, src), [], [out], 60.0, "dma", late=LOAD, after=dmas.get(q))
 
     def store(q, dst, src, reg):
         op(q, lambda: dq[q].dma_start(dst, src), [reg], [], 60.0, "dma", late=LOAD)
 
     def iota(out, pattern, base, mult):
         cost = 130 + 2 * CY * wide(out)
-        if out[0] in ("KI", "CJ"):
+        if SCRATCH[out[0]][2] == F32:
             op("g", lambda: g.iota(ap(out), pattern, base, mult, allow_small_or_imprecise_dtypes=True), [], [out], cost)
         else:
             op("g", lambda: g.iota(ap(out), pattern, base, mult), [], [out], cost)
 
-    load("sy", ("X", PAD + 4 * A, PAD + 4 * H), T.x[:, 4 * A:4 * H])
+    def x(lo, hi, lane=None):
+        return ("X", PAD + 4 * lo, PAD + 4 * hi) if lane is None else ("X", PAD + 4 * lo + lane, PAD + 4 * hi, 4)
+
+    load("sy", x(A, H), T.x[:, 4 * A:4 * H])
     load("a", ("ut", 0, 512), T.u[:, :])
-    load("sy", ("X", PAD + 4 * H, PAD + 4 * C), T.x[:, 4 * H:4 * C])
-    load("sy", ("X", PAD, PAD + 4 * A), T.x[:, 0:4 * A])
+    load("sy", x(H, C), T.x[:, 4 * H:4 * C])
+    load("sy", x(0, A), T.x[:, 0:4 * A])
     load("sy", ("WQ", 0, 512), T.wc[:, :])
     load("sy", ("WS", 0, 512), T.ws[:, :])
     load("sy", ("vt", 0, 512), T.v[:, :])
 
     iota(("pi", 0, 1), [[1, 1]], 0, 1)
-    iota(("m16", 0, NE), [[16, NE]], 0, 0)
-    iota(("ulist", 0, 8), [[16, 8]], 0, 0)
-    iota(("ulist", 8, 16), [[16, 8]], 1, 0)
-    iota(("KI", 0, 520), [[1, 520]], -3, -4)
-    fill(("low", 0, 72), -1.0e29)
+    iota(("KI", 0, 128), [[1, 128]], 0, -1)
+    iota(("m16", 0, 28), [[16, 28]], 0, 0)
+    iota(("ulist", 0, 16), [[1, 2], [16, 8]], 0, 0)
+    iota(("mp", 0, 2 * NP), [[CUT, 2], [16, NP]], 0, 0)
+    iota(("mj", 0, 2 * NC), [[0, 2], [16, NC]], 0, 0)
+    low = ("low", 0, 96)
+    fill(low, -1.0e29)
+    fill(("EH", 0, 528), 0.0)
+    ts(("EH", 3, 515, 4), ("KI", 0, 128), 0.0, M.is_equal, 0.5, M.mult)
+    lin("a", ("EB", 0, 520), ("EH", 0, 520), 64.0, 0.0)
     ts(("pa", 0, 1), ("pi", 0, 1), 15, M.bitwise_and)
-    cp(("pf", 0, 1), ("pa", 0, 1))
+    pf = ("pf", 0, 1)
+    cp(pf, ("pa", 0, 1))
     fill(("X", 0, PAD), 0.0)
     fill(("Bt", 4 * K, 512), 0.0)
-    ts(("ei", 0, NE), ("m16", 0, NE), ("pf", 0, 1), M.add)
-    ts(("ti", 0, NE), ("ei", 0, NE), 3, M.bitwise_and)
-    ts(("ji", 0, NE), ("ei", 0, NE), 2, M.arith_shift_right)
-    cp(("TT", 0, NE), ("ti", 0, NE))
-    cp(("J", 0, NE), ("ji", 0, NE))
-    cp(("EF", 0, NE), ("ei", 0, NE))
-    ts(("EQ", 0, 12), ("ei", 16, 28), 0.25, M.mult, -64.0, M.add)
-    ts(("ET0", 0, 28), ("ei", 0, 28), 0.25, M.mult, 52.0, M.add)
-    ts(("ET2", 0, 12), ("ei", 16, 28), 0.25, M.mult, 180.0, M.add)
-    m4 = ts(None, ("J", 0, NE), -4.0, M.mult)
-    tt(("AM", 0, NE), m4, ("TT", 0, NE), M.add)
-    ts(("ET3", 0, 12), ("AM", 16, 28), 0.25, M.mult, 51.0, M.add)
-    cp(("J", NE, NL), ("ei", 0, NL - NE))
-    fill(("TT", NE, NL), 0.0)
-    for t, f in (("CK", lambda e: e[2]), ("C0", lambda e: e[3] + L1 * e[1] + L2 * e[2]), ("CC", lambda e: e[1])):
-        def put(i, j, x, t=t):
-            if t == "CK":
-                fill((t, i, j), x)
-            else:
-                act((t, i, j), ("low", i, j), AF.Identity, bias=x, scale=0.0)
-        put(0, NS, 0.0)
+    cp(("uoff", 0, 16), ("ulist", 0, 16))
+    zs = ("ZS", 0, 336)
+    SV, B0, N0, R0, R1 = ("ZS", 0, 4 * NS), ("ZS", 64, 100), ("ZS", 100, 100 + 4 * NJ), ("ZS", 192, 192 + 4 * NC), ("ZS", 264, 264 + 4 * NC)
+    B1, W1, U1, U2, N1, PAT = ("B1", 0, 36), ("W1", 0, 4 * NA), ("U1", 0, 2 * NA), ("U2", 0, 2 * NA), ("N1", 0, 4 * NJ), ("PAT", 0, 4 * NA)
+    fill(zs, 0.0)
+    fill(PAT, 1.0, "v")
+    fill(slot(PAT, 0), 0.0, "v")
+    fill(slot(PAT, 1), -1.0, "v")
+    ts(("ei", 0, 28), ("m16", 0, 28), pf, M.add)
+    ts(("zi", 0, 12), ("ei", 16, 28), 2, M.arith_shift_right)
+    ZQ, NZ, ET = ("ZQ", 0, 12), ("NZ", 0, 12), ("ET", 0, 16)
+    ts(ZQ, ("zi", 0, 12), L2 + 0.5, M.add)
+    ts(NZ, ("zi", 0, 12), -1.0, M.mult, float(C - L1 - L2), M.add)
+    ts(slot(B1, 1, 3), ("zi", 0, 12), -2.0, M.mult, -1.0, M.add)
+    ts(ET, ("ei", 0, 16), 0.25, M.mult, L1 - L2 + PAD / 4, M.add)
+    ts(slot(B1, 2, 3), ("ei", 16, 28), 0.25, M.mult, L1 - L2 + PAD / 4, M.add)
+    PL, PB, J, J2, J6 = ("PL", 0, NA), ("PB", 0, NA), ("J", 0, NJ), ("J2", 0, NJ), ("J6", 0, NJ)
+    lin("a", PL, ("mp", 0, NA), 1.0, pf)
+    lin("a", J, ("mj", 0, NJ), 1.0, pf)
+    lin("a", PB, PL, -2048.0, 0.0)
+    lin("a", slot(W1, 1), PL, -1.0, 0.0)
+    fill(slot(U1, 0, 2), BIG, "a")
+    fill(slot(U2, 0, 2), -BIG, "a")
+    lin("a", J2, J, 0.5, 0.0)
+    lin("a", J6, J, -1.0 / 6.0, 0.0)
+    fill(slot(N0, 0), -BIG, "a")
+    lin("a", slot(N0, 3), J, 0.5, -0.35)
+    lin("a", slot(N1, 0), J, -0.25, 0.0)
+    fill(slot(N1, 3), -BIG, "a")
+    for t, f in (("CK", lambda e: e[2]), ("CC", lambda e: e[1])):
+        fill((t, 0, NS), 0.0, "v")
         i = 0
-        while i < len(SCAL):
+        while i < NS:
             j = i
-            while j < len(SCAL) and f(SCAL[j]) == f(SCAL[i]):
+            while j < NS and f(SCAL[j]) == f(SCAL[i]):
                 j += 1
             if f(SCAL[i]) != 0.0:
-                put(i, j, float(f(SCAL[i])))
+                fill((t, i, j), float(f(SCAL[i])), "v" if t == "CC" else "a")
             i = j
-    act(("S4", 0, NE), ("J", 0, NE), AF.Identity, bias=2.0, scale=4.0)
-    act(("J4", 0, NL), ("J", 0, NL), AF.Copy, scale=0.25)
-    act(("TM", 0, NE), ("TT", 0, NE), AF.Identity, bias=-898.0)
-    cp(("uoff", 0, 16), ("ulist", 0, 16))
-    ts(("EH", 0, 520), ("KI", 0, 520), 0.0, M.is_equal, 0.5, M.mult)
-    act(("EB", 0, 520), ("EH", 0, 520), AF.Copy, scale=64.0)
+    for i, e in enumerate(SCAL):
+        fill(("ZS", 4 * i, 4 * i + 1), -(e[3] + L1 * e[1] + L2 * e[2]), "a")
 
     quant("QU", "SU", 0, 128, ("ut", 0, 512))
     op("v", lambda: g.vector.tensor_copy(T.QUU[:, 0:256].bitcast(dt.uint32), T.QU[:, 0:128].bitcast(dt.uint32).indirect(T.uoff[:, 0:16])),
@@ -333,36 +518,29 @@ def rank_program(g, core, T, topo):
     for r in range(ROUNDS):
         last = r == ROUNDS - 1
         qx, sx, qb, sb, lb, la, lx = ["%s%d" % (s, r) for s in ("QX", "SX", "QB", "SB", "lb", "la", "lx")]
-        quant("QS", "SS", 0, 128, ("X", PAD + 4 * A, PAD + 4 * H))
-        mm(1, 128, "QUU", "SUU", 128, "QS", "SS", 0)
-        mm(0, 128, "QUU", "SUU", 0, "QS", "SS", 0)
+        quant("QS", "SS", 0, 128, x(A, H))
+        mm(4, 128, "QUU", "SUU", 0, "QS", "SS", 0, after=mm(5, 128, "QUU", "SUU", 128, "QS", "SS", 0))
 
-        def first(bank, lo, n):
-            run, m, out = new(n), new(n), new(1)
+        def first(bank, lo, n, after):
+            m, out = new(n), new(1)
+            run = scan(None, ("P%d" % bank, lo, lo + n), ("low", 0, n), M.max, M.max, -1.0e29)
             top = ("WK", run[2] - 1, run[2])
-            op("v", lambda: g.vector.tensor_tensor_scan(ap(run), T["P%d" % bank][:, lo:lo + n], T.low[:, 0:n], -1.0e29, M.max, M.max),
-               [("P%d" % bank, 0, 512), ("low", 0, 72)], [run], CY * max(64, n))
-            op("a", lambda: g.scalar.activation(ap(m), ap(run), AF.Sign, bias=ap(top), scale=-1.0, accum_out=ap(out)), [run], [m, out], 100.0)
-            return out
-        kk = first(1, L2 - A, H2 - L2 + 1)
-        cc = first(0, L1 - A, H1 - L1 + 1)
+            return out, op("a", lambda: g.scalar.activation(ap(m), ap(run), AF.Sign, bias=ap(top), scale=-1.0, accum_out=ap(out)), [run], [m, out],
+                           100.0, after=after)
+        kk, i = first(5, L2 - A, H2 - L2 + 1, None)
+        cc, i = first(4, L1 - A, H1 - L1 + 1, i)
         xs = ("X", 0, PAD + 4 * C)
-        b5 = ts(None, ("ET0", 0, 16), cc, M.add, kk, M.subtract)
-        ts((lb, 0, 16), b5, 4.0, M.mult)
-        gather("a", ("Bt", 0, 256), xs, (lb, 0, 16))
-        b0 = ts(None, ("EQ", 0, 12), kk, M.is_lt)
-        b1 = ts(None, ("EQ", 0, 12), kk, M.is_ge, C + 4.0, M.mult)
-        b2 = ts(None, ("ET0", 16, 28), cc, M.add, kk, M.subtract)
-        b3 = ts(None, ("ET2", 0, 12), cc, M.add, kk, M.add)
-        b4 = ts(None, ("ET3", 0, 12), cc, M.add, kk, M.subtract)
-        b1 = tt(None, b3, b1, M.is_lt)
-        b2 = tt(None, b2, b0, M.mult)
-        b3 = tt(None, b3, b1, M.mult)
-        b2 = tt(None, b2, b4, M.max)
-        b2 = tt(None, b2, b3, M.max)
-        ts((lb, 16, 28), b2, 4.0, M.mult)
-        gather("a", ("Bt", 352, 448), xs, (lb, 22, 28))
+        ts(slot(B1, 0, 3), ZQ, kk, M.add, 2.0, M.mult)
+        ts(slot(B0, 2, 3), ZQ, -2.0 * L2 - 0.5, M.add, kk, M.is_ge)
+        ts(slot(B0, 1, 3), NZ, cc, M.subtract, kk, M.is_gt)
+        dd = lin("v", None, kk, -1.0, cc)
+        bs = scan(None, B0, B1, M.mult, M.add)
+        ts((lb, 0, 16), ET, dd, M.add, 4.0, M.mult)
+        ts((lb, 16, 28), slot(bs, 2, 3), dd, M.add, 4.0, M.mult)
+        gather("a", ("Bt", 0, 160), xs, (lb, 0, 10))
+        gather("v", ("Bt", 160, 256), xs, (lb, 10, 16))
         gather("v", ("Bt", 256, 352), xs, (lb, 16, 22))
+        gather("a", ("Bt", 352, 448), xs, (lb, 22, 28))
         quant(qb, sb, 0, 128, ("Bt", 0, 512))
         rid, pid = topo.addr(to, core)
         mask = topo.mask(core, to)
@@ -374,112 +552,97 @@ def rank_program(g, core, T, topo):
         if r == 0:
             for b in range(4):
                 quant("QEH", "SEH", 128 * b, 128, ("EH", 3 - b, 515 - b))
-        quant(qx, sx, 0, C, ("X", PAD, PAD + 4 * C))
+        quant(qx, sx, 0, C, x(0, C))
         for b in range(4):
-            mm(4 + b, C, "QEH", "SEH", 128 * b, qx, sx, 0)
-        sa1 = ts(None, ("CC", 0, NS), cc, M.mult)
-        sa2 = ts(None, ("CK", 0, NS), kk, M.mult)
-        sa3 = tt(None, sa2, ("C0", 0, NS), M.add)
-        sv = tt(None, sa1, sa3, M.add)
-        sc = {e[0]: ("WK", sv[1] + i, sv[1] + i + 1) for i, e in enumerate(SCAL)}
-        EF, S4 = ("EF", 0, NE), ("S4", 0, NE)
-        s0 = act(None, S4, AF.Abs, bias=sc["nmid4"])
-        s1 = act(None, S4, AF.Abs, bias=sc["nc4"])
-        s2 = act(None, s1, AF.Abs, bias=sc["nk4"])
-        for b in range(4):
-            act(("FG", 0, 4 * C, b), ("P%d" % (4 + b), 0, C), AF.Copy)
-            act(("FO", 0, 4 * CUT, b), ("P%d" % (4 + b), 0, CUT), AF.Copy)
-        w0 = ts(None, ("AM", 0, NE), sc["c8"], M.add)
-        w2 = ts(None, EF, sc["n34"], M.is_lt, 1152.0, M.mult)
-        alt = ts(None, EF, sc["m8k"], M.add)
-        w1 = ts(None, s0, sc["kh4"], M.is_lt, sc["k8"], M.mult)
-        zt = tt(None, s2, ("TM", 0, NE), M.add)
-        w0 = tt(None, w0, w2, M.add)
-        w0 = tt(None, w0, w1, M.add)
-        w4 = ts(None, w0, 1152.0, M.is_lt, 4096.0, M.mult)
-        w4 = tt(None, w4, alt, M.add)
-        w0 = tt(None, w0, w4, M.min)
-        w5 = ts(None, w0, 0.0, M.is_lt, 2048.0, M.mult)
-        w5 = tt(None, w5, zt, M.add)
-        w0 = tt(None, w0, w5, M.max)
-        cp((la, 0, NE), w0)
-        for b in range(4):
-            mm(b, C - CUT, "QEH", "SEH", 128 * b, qx, sx, CUT)
-            act(("FB", 0, 4 * (C - CUT), b), ("P%d" % b, 0, C - CUT), AF.Copy, scale=64.0)
+            mm(b, C, "QEH", "SEH", 128 * b, qx, sx, 0)
+            cp(("FG", FW * b, FW * b + C), ("P%d" % b, 0, C), "a")
+            cp(("FO", CUT * b, CUT * b + CUT), ("FG", FW * b, FW * b + CUT), "v")
         if r == 0:
             for b in range(4):
                 quant("QEB", "SEB", 128 * b, 128, ("EB", 3 - b, 515 - b))
-        n = NL if last else NE
-        J, zi = ("J", 0, n), ("oi%d" % r, 0, n)
-        aa = tt(None, sc["n2"], sc["n3"], M.min)
-        hh = tt(None, sc["k2"], sc["h2"], M.min)
-        p0 = ts(None, J, aa, M.subtract, 1.0 / 3.0, M.mult)
-        p1 = ts(None, J, hh, M.subtract, 0.5, M.mult)
-        p2 = ts(None, J, aa, M.subtract, sc["k2"], M.subtract)
-        p0 = tt(None, p0, ("J4", 0, n), M.max)
-        p1 = tt(None, p1, p2, M.max)
-        p0 = tt(None, p0, p1, M.max)
-        ts(zi, p0, -0.35, M.add)
-        fr = tt(None, p0, zi, M.subtract)
-        mk = ts(None, zi, sc["k"], M.is_ge, 0.55, M.mult)
-        ov = ts(None, zi, sc["n2"], M.is_ge, 0.17, M.mult)
-        z2 = ts(None, zi, 2.0, M.mult, 1.0, M.add)
-        tc = ts(None, ("TT", 0, n), sc["c4"], M.add)
-        y = tt(None, fr, mk, M.add)
-        mo = tt(None, mk, ov, M.add)
-        ta = ts(None, y, 0.45, M.is_ge, 0.5, M.subtract)
-        y2 = tt(None, fr, mo, M.add)
-        y2 = act(None, y2, AF.Abs, bias=-0.45)
-        t = tt(None, ta, z2, M.mult)
-        u = ts(None, t, sc["k"], M.add, 8.0, M.mult)
-        sg = ts(None, y2, 0.25, M.is_lt, 0.5, M.subtract)
-        f = tt(None, u, sg, M.mult)
-        f = tt(None, f, tc, M.add)
-        cp((lx, 0, n), f)
-        if last:
-            iota(("CJ", 0, 4 * C), [[1, C], [0, 4]], 0, 0)
-            quant("QV", "SV", 0, 128, ("vt", 0, 512))
-        came = op("t", lambda r=r: g.tensor.wait_ge(T.sem["came%d" % r], 2 * len(topo.engines(frm, core))), [], [], 0.0, "wait", after=sent)
-        for b in range(4):
-            mm(4 + b, 128, "QEH", "SEH", 128 * b, qx, sx, C + K - 128, after=came)
-        for b in range(4):
-            out, src = ("FG", 4 * C, 4 * (C + K), b), ("P%d" % (4 + b), 128 - K, 128)
-            if b % 2:
-                act(out, src, AF.Copy)
-            else:
-                cp(out, src)
         for b in range(4):
             mm(4 + b, CUT, "QEB", "SEB", 128 * b, qx, sx, 0, True, False)
-        win = ("FG", 0, 4 * (C + K))
-        gather("a", ("AN", 0, 4 * (C - CUT)), win, (la, CUT // 4, C // 4))
-        off, own, out = (la, 0, CUT // 4), ("FO", 0, 4 * CUT), ("Z", 0, 4 * CUT)
-        op("v", lambda off=off, own=own, out=out: tt_(ap(out), ap(win).indirect(ap(off)), ap(own), M.add), [win, off, own], [out], 50 + 1.5 * CY * 4 * CUT)
-        quant("QZ", "SZ", 0, CUT, out)
+        lin("a", slot(SV, 2), ("CK", 0, NS), kk, 0.0)
+        lin("a", slot(SV, 1), ("CC", 0, NS), cc, 0.0)
+        sv = scan(None, ("PAT", 0, 4 * NS), SV, M.mult, M.add)
+        sc = {e[0]: ("WK", sv[1] + 4 * i + 3, sv[1] + 4 * i + 4) for i, e in enumerate(SCAL)}
+        ts(slot(W1, 0), PL, sc["s"], M.is_ge, sc["k2"], M.mult)
+        ts(slot(W1, 3), PL, sc["cm"], M.is_ge, sc["k2"], M.mult)
+        ts(slot(W1, 2), PB, sc["fb"], M.add, sc["c2"], M.max)
+        a1 = act(None, PL, AF.Abs, bias=sc["cm"], scale=-1.0)
+        w = scan(None, PAT, W1, M.mult, M.add)
+        ts(slot(U1, 1, 2), slot(w, 3), 0.5, M.is_lt, 4096.0, M.mult)
+        lin("a", slot(w, 1), PL, 1.0, sc["nalt"])
+        w = scan(None, U1, slot(w, 1, 2), M.add, M.min)
+        ts(slot(U2, 1, 2), slot(w, 1, 2), -287.5, M.is_ge, -4096.0, M.mult)
+        act(slot(w, 0, 2), a1, AF.Abs, bias=sc["nk"])
+        w = scan(None, U2, w, M.add, M.max)
+        ts((la, 0, NA), slot(w, 1, 2), 287.5, M.add)
+        j0 = 0 if last else A // 16
+        n0, n1 = (N0[0], N0[1] + 4 * j0, N0[1] + 4 * (j0 + NC)), (N1[0], 4 * j0, 4 * (j0 + NC))
+        o = sc["a1"][1]
+        ln = tt(None, ("WK", o, o + 9, 4), ("WK", o + 12, o + 21, 4), M.max)
+        ln = [("WK", ln[1] + i, ln[1] + i + 1) for i in range(3)]
+        ts(slot(n1, 1), ("J6", j0, j0 + NC), ln[0], M.add, ln[1], M.max)
+        lin("a", slot(n1, 2), ("J2", j0, j0 + NC), 1.0, ln[2])
+        o = new(4 * NC + 4)
+        hi = slot(scan((o[0], o[1], o[2] - 4), n0, n1, M.add, M.max), 3)
+        o = (o[0], o[1] + 1, o[2] - 3)
+        ts(slot(o, 0), hi, WHOLE, M.add, -WHOLE, M.add)
+        ts(slot(R1, 0), hi, WHOLE, M.add, -WHOLE, M.add)
+        ts(slot(o, 1), hi, sc["kh"], M.is_ge, 0.55, M.mult)
+        ts(slot(o, 3), hi, sc["n2h"], M.is_ge, 0.17, M.mult)
+        y = scan(None, ("PAT", 0, 4 * NC), o, M.mult, M.add)
+        act(slot(R0, 1), slot(y, 2), AF.Sign, bias=-0.10)
+        ts(slot(R1, 1), slot(y, 2), 0.10, M.is_ge, sc["kh"], M.add)
+        act(slot(R0, 2), slot(y, 3), AF.Sign, bias=0.14)
+        act(slot(R0, 3), slot(y, 3), AF.Sign, bias=0.35, scale=-1.0)
+        y = scan(None, R0, R1, M.mult, M.add)
+        ts((lx, 0, NC), slot(y, 3), sc["cm"], M.add)
+        if last:
+            iota(("CJ", 0, C), [[1, C]], 0, 0)
+            quant("QV", "SV", 0, 128, ("vt", 0, 512))
+            gather("a", ("LO", 0, C), ("CJ", 0, C), (lx, 0, NC))
+        came = op("t", lambda r=r: g.tensor.wait_ge(T.sem["came%d" % r], 2 * len(topo.engines(frm, core))), [], [], 0.0, "wait", after=sent)
+        n2 = C - CUT
+        for b in range(4):
+            mm(b, 128, "QEH", "SEH", 128 * b, qx, sx, C + K - 128, after=came)
+        for b in range(4):
+            cp(("FG", FW * b + C, FW * b + FW), ("P%d" % b, 128 - K, 128), "av"[b % 2])
+        for b in range(4):
+            mm(b, n2, "QEB", "SEB", 128 * b, qx, sx, CUT, True, False)
+        for b in range(4):
+            win = ("FG", FW * b, FW * b + FW)
+            gather("a", ("AN", n2 * b, n2 * b + n2), win, (la, NP, NA))
+            off, own, out = (la, 0, CUT // 16), ("FO", CUT * b, CUT * b + CUT), ("Z", b, 4 * CUT, 4)
+            op("v", lambda win=win, off=off, own=own, out=out: tt_(ap(out), ap(win).indirect(ap(off)), ap(own), M.add), [win, off, own], [out], 50 + 1.5 * CY * CUT)
+        quant("QZ", "SZ", 0, CUT, ("Z", 0, 4 * CUT))
         for b in range(4):
             mm(4 + b, CUT, "WQ", "WS", 128 * b, "QZ", "SZ", 0, False, True)
         for b in range(4):
-            tt(("Z", 4 * CUT, 4 * C, b), ("P%d" % b, 0, C - CUT), ("AN", 0, 4 * (C - CUT), b), M.add)
-        quant("QZ", "SZ", CUT, C - CUT, ("Z", 4 * CUT, 4 * C))
+            tt(("Z", 4 * CUT + b, 4 * C, 4), ("P%d" % b, CUT, C), ("AN", n2 * b, n2 * b + n2), M.add)
+        quant("QZ", "SZ", CUT, n2, ("Z", 4 * CUT, 4 * C))
         for b in range(4):
-            mm(b, C - CUT, "WQ", "WS", 128 * b, "QZ", "SZ", CUT)
+            mm(b, n2, "WQ", "WS", 128 * b, "QZ", "SZ", CUT, False, True)
         for b in range(4):
-            act(("Y", 0, 4 * CUT, b), ("P%d" % (4 + b), 0, CUT), AF.Copy)
+            cp(("Y", C * b, C * b + CUT), ("P%d" % (4 + b), 0, CUT), "a")
         for b in range(4):
-            tt(("Y", 4 * CUT, 4 * C, b), ("P%d" % b, 0, C - CUT), ("FB", 0, 4 * (C - CUT), b), M.add)
-        y, x = ("Y", 0, 4 * C), lambda lo, hi: ("X", PAD + 4 * lo, PAD + 4 * hi)
+            cp(("Y", C * b + CUT, C * b + C), ("P%d" % b, 0, n2), "va"[b % 2])
         if not last:
-            for q, lo, hi in (("v", A, MID), ("a", MID, H), ("a", H, C), ("a", 0, A)):
-                gather(q, x(lo, hi), y, (lx, lo // 4, hi // 4), 0.03125)
+            for b in range(4):
+                gather("va"[b % 2], x(A, H, b), ("Y", C * b, C * b + C), (lx, 0, (H - A) // 16), 0.03125)
+            for b in range(4):
+                gather("vaaa"[b], x(H, C + A, b), ("Y", C * b, C * b + C), (lx, (H - A) // 16, NC), 0.03125)
+            cp(x(0, A), x(C, C + A), "v")
             continue
+        for b in range(4):
+            gather("va"[b % 2], x(0, C, b), ("Y", C * b, C * b + C), (lx, 0, NC), 0.03125)
         cut = 144
-        for q, lo, hi in (("v", 0, cut), ("a", cut, C)):
-            gather(q, x(lo, hi), y, (lx, lo // 4, hi // 4), 0.03125)
         for i, (lo, hi) in enumerate(((0, cut), (cut, C))):
             quant("QL", "SL", lo, hi - lo, x(lo, hi))
-            mm(i, hi - lo, "QV", "SV", 0, "QL", "SL", lo)
-        gather("a", ("LO", 0, C), ("CJ", 0, 4 * C), (lx, NE, NL))
-        cp(("yt", 0, cut), ("P0", 0, cut))
-        cp(("yt", cut, C), ("P1", 0, C - cut))
+            mm(4 + i, hi - lo, "QV", "SV", 0, "QL", "SL", lo)
+        cp(("yt", 0, cut), ("P4", 0, cut), "v")
+        cp(("yt", cut, C), ("P5", 0, C - cut), "v")
         store("sy", T.oc[:, :], T.QL[:, 0:C].bitcast(dt.uint8), ("QL", 0, C))
         for k in range(4):
             store("a", T.osc[4 * k:4 * k + 4, 0:C], T.SL[32 * k:32 * k + 4, 0:C], ("SL", 0, C))

import math
from concourse.mybir import dt, AluOpType, AxisListType, ActivationFunctionType

C, K, ROUNDS = 288, 112, 3
L1, H1, L2, H2 = 112, 176, 64, 96
A, H = 64, 192
PAD = 16
CUT = 144
NC = C // 16
NP = CUT // 16 + CUT // 16 % 2
NA = NP + (C - CUT) // 16
NJ = NC + A // 16
FW = C + K
NW = 4096
BIG = 65536.0
WHOLE = 12582912.0

SCAL = [("fb", 2048.0, -2048.0, -1024.0), ("c2", 2.0, 0.0, -288.5), ("cm", 1.0, 0.0, -0.5), ("s", 1.0, 1.0, -0.5), ("n2h", -1.0, -1.0, 287.5),
        ("k2", 0.0, 2.0, 0.0), ("nalt", 0.0, -2.0, -287.5), ("kh", 0.0, 1.0, -0.5),
        ("a1", 1.0 / 3.0, 1.0 / 3.0, -96.0), ("nk", 0.0, -1.0, 0.0), ("c1", 1.0, -1.0, -288.0),
        ("a2", -1.0 / 3.0, 1.0 / 3.0, 0.0), ("b2", 0.0, 1.0, -144.12), ("c3", -1.0, -1.0, 0.0)]
NS = len(SCAL)

F32, BF, I32, U16, U8, X4 = "float32", "bfloat16", "int32", "uint16", "uint8", "float8_e4m3fn_x4"
SCRATCH = {
    "X": ("sbuf", [128, PAD + 4 * (C + A)], BF), "Bt": ("sbuf", [128, 512], BF), "Z": ("sbuf", [128, 4 * C], BF),
    "Y": ("sbuf", [128, 4 * C], BF), "FG": ("sbuf", [128, 4 * FW], BF), "AN": ("sbuf", [128, 4 * (C - CUT)], BF),
    "FO": ("sbuf", [128, 4 * CUT], BF),
    "ut": ("sbuf", [128, 512], BF), "vt": ("sbuf", [128, 512], BF),
    "QU": ("sbuf", [128, 128], X4), "SU": ("sbuf", [128, 128], U8), "QUU": ("sbuf", [128, 256], X4), "SUU": ("sbuf", [128, 256], U8),
    "QV": ("sbuf", [128, 128], X4), "SV": ("sbuf", [128, 128], U8),
    "WQ": ("sbuf", [128, 512], X4), "WS": ("sbuf", [128, 512], U8),
    "QS": ("sbuf", [128, 128], X4), "SS": ("sbuf", [128, 128], U8),
    "QZ": ("sbuf", [128, C], X4), "SZ": ("sbuf", [128, C], U8),
    "QL": ("sbuf", [128, C], X4), "SL": ("sbuf", [128, C], U8),
    "EH": ("sbuf", [128, 528], BF), "EB": ("sbuf", [128, 528], BF), "KI": ("sbuf", [128, 128], F32),
    "QEH": ("sbuf", [128, 512], X4), "SEH": ("sbuf", [128, 512], U8), "QEB": ("sbuf", [128, 512], X4), "SEB": ("sbuf", [128, 512], U8),
    "pi": ("sbuf", [128, 1], I32), "pa": ("sbuf", [128, 1], I32), "pf": ("sbuf", [128, 1], F32),
    "m16": ("sbuf", [128, 28], I32), "ei": ("sbuf", [128, 28], I32), "zi": ("sbuf", [128, 12], I32),
    "mp": ("sbuf", [128, 2 * NP], F32), "mj": ("sbuf", [128, 2 * NC], F32), "PL": ("sbuf", [128, NA], F32), "J": ("sbuf", [128, NJ], F32),
    "PB": ("sbuf", [128, NA], F32), "J2": ("sbuf", [128, NJ], F32), "J6": ("sbuf", [128, NJ], F32),
    "ZQ": ("sbuf", [128, 12], F32), "NZ": ("sbuf", [128, 12], F32), "ET": ("sbuf", [128, 16], F32),
    "low": ("sbuf", [128, 96], F32),
    "ulist": ("sbuf", [128, 16], I32), "uoff": ("sbuf", [128, 16], U16),
    "CC": ("sbuf", [128, NS], F32), "CK": ("sbuf", [128, NS], F32),
    "PAT": ("sbuf", [128, 4 * NA], F32), "ZS": ("sbuf", [128, 336], F32), "B1": ("sbuf", [128, 36], F32), "W1": ("sbuf", [128, 4 * NA], F32),
    "U1": ("sbuf", [128, 2 * NA], F32), "U2": ("sbuf", [128, 2 * NA], F32), "N1": ("sbuf", [128, 4 * NJ], F32),
    "CJ": ("sbuf", [128, C], F32), "LO": ("sbuf", [128, C], F32), "yt": ("sbuf", [128, C], F32),
    "WK": ("sbuf", [128, NW], F32),
}
for _i in range(8):
    SCRATCH["P%d" % _i] = ("psum", [128, 512], F32)
for _i in range(ROUNDS):
    SCRATCH["QX%d" % _i] = ("sbuf", [128, C + K], X4)
    SCRATCH["SX%d" % _i] = ("sbuf", [128, C + K], U8)
    SCRATCH["QB%d" % _i] = ("sbuf", [128, 128], X4)
    SCRATCH["SB%d" % _i] = ("sbuf", [128, 128], U8)
    SCRATCH["lb%d" % _i] = ("sbuf", [128, 28], U16)
    SCRATCH["la%d" % _i] = ("sbuf", [128, NA + 1], U16)
    SCRATCH["lx%d" % _i] = ("sbuf", [128, NC], U16)
DMAS = ["d%d" % i for i in range(24)]
SEMAPHORES = ["ev", "ea", "et", "eg"] + DMAS + ["gone"] + ["came%d" % i for i in range(ROUNDS)]
BACK = 180.0
EXCHANGE, LOAD = 1800.0, 1900.0
FIGURES = [(140.0, 1400.0, 1800.0, 1.0), (200.0, 2200.0, 2000.0, 1.0), (170.0, 1800.0, 1900.0, 1.3)]
TRIES, SLACK, SEED, EARLY = 40000, 100.0, 12345, 0.5
plan = {}


def planner(g, T):
    queue = {"v": g.vector, "a": g.scalar, "t": g.tensor, "g": g, "sy": g.sync}
    sem_of = {"v": "ev", "a": "ea", "t": "et", "g": "eg"}
    nodes, log = [], {}

    def bank(r):
        return SCRATCH[r[0]][0] == "psum"

    def norm(r):
        if bank(r):
            return (r[0], 0, 512, 1)
        return r if len(r) == 4 else r + (1,)

    def hits(x, y):
        return x[1] < y[2] and y[1] < x[2] and (x[1] - y[1]) % math.gcd(x[3], y[3]) == 0

    def covers(x, y):
        return x[1] <= y[1] and y[2] <= x[2] and y[3] % x[3] == 0 and (y[1] - x[1]) % x[3] == 0

    def op(q, call, reads, writes, cost, kind="op", acc=False, after=None, late=0.0, other=None):
        reads = [norm(r) for r in reads]
        writes = [norm(r) for r in writes]
        deps, soft = set(), set()
        for regs, wr in ((reads, False), (writes, True)):
            for r in regs:
                for (o, reg, w) in log.get(r[0], []):
                    if (wr or w or bank(r)) and hits(r, reg):
                        (soft if acc and nodes[o]["q"] == "t" and w and wr else deps).add(o)
        if after is not None:
            soft.add(after)
        i = len(nodes)
        nodes.append({"q": q, "call": call, "deps": deps, "soft": soft - deps, "cost": cost, "kind": kind, "ways": [(q, call, cost), other], "late": late})
        for r in writes:
            log[r[0]] = [e for e in log.get(r[0], []) if acc or not covers(r, e[1])]
            log[r[0]].append((i, r, True))
        for r in reads:
            log.setdefault(r[0], []).append((i, r, False))
        return i

    def order():
        n = len(nodes)
        if n in plan:
            return plan[n]
        pre = [[(p, BACK + nodes[p]["late"]) for p in sorted(d["deps"])] + [(p, nodes[p]["late"] * (nodes[p]["kind"] == "send")) for p in sorted(d["soft"])]
               for d in nodes]
        cost = [d["cost"] for d in nodes]
        prio = [c + d["late"] for c, d in zip(cost, nodes)]
        for i in range(n - 1, -1, -1):
            for p, b in pre[i]:
                prio[p] = max(prio[p], cost[p] + b + prio[i])
        left = [len(x) for x in pre]
        out = [[] for _ in nodes]
        for i in range(n):
            for p, b in pre[i]:
                out[p].append(i)
        free = {q: 0.0 for q in queue}
        todo = {q: [i for i in range(n) if nodes[i]["q"] == q] for q in queue}
        est, end, seq = [0.0] * n, [None] * n, []
        while len(seq) < n:
            for i in range(n):
                if end[i] is None:
                    e = free[nodes[i]["q"]]
                    for p, b in pre[i]:
                        x = (est[p] + cost[p] if end[p] is None else end[p]) + b
                        if x > e:
                            e = x
                    est[i] = e
            best = spare = None
            for q in queue:
                can = [i for i in todo[q] if not left[i]]
                if not can:
                    continue
                s = min(est[i] for i in can)
                pick = max((i for i in can if est[i] <= s + 1.0), key=lambda i: prio[i])
                if spare is None or est[pick] < est[spare]:
                    spare = pick
                for i in sorted(can, key=lambda i: est[i] - 0.001 * prio[i]):
                    hold = False
                    for m in todo[q]:
                        if m != i and prio[m] > prio[i] and est[m] < est[i] + cost[i]:
                            if max(est[i] + prio[i], est[i] + cost[i] + prio[m]) > max(est[m] + prio[m], est[m] + cost[m] + prio[i]):
                                hold = True
                                break
                    if not hold:
                        if best is None or est[i] < est[best]:
                            best = i
                        break
            pick = spare if best is None else best
            end[pick] = est[pick] + cost[pick]
            free[nodes[pick]["q"]] = end[pick]
            todo[nodes[pick]["q"]].remove(pick)
            seq.append(pick)
            for j in out[pick]:
                left[j] -= 1
        seq = polish(seq)
        plan[n] = seq
        return seq

    def polish(seq):
        n = len(nodes)
        names = list(queue)
        qs, way, cost = [names.index(d["q"]) for d in nodes], [0] * n, [d["cost"] for d in nodes]
        two = [i for i in range(n) if nodes[i]["ways"][1]]
        before = [set(d["deps"]) | set(d["soft"]) for d in nodes]
        sets = []
        for back, exchange, load, slow in FIGURES:
            late = [exchange if d["kind"] == "send" else load if d["kind"] == "dma" else 0.0 for d in nodes]
            sets.append(([[(p, back + late[p]) for p in sorted(d["deps"])] + [(p, late[p] * (nodes[p]["kind"] == "send")) for p in sorted(d["soft"])]
                          for d in nodes],
                         [slow if d["kind"] == "op" else 1.0 for d in nodes], [load if d["kind"] == "dma" else 0.0 for d in nodes]))

        def run(s, fig):
            pre, slow, tail = fig
            free, last = [0.0] * len(queue), [-1] * len(queue)
            end, why, top, at = [0.0] * n, [-1] * n, 0.0, -1
            for i in s:
                q = qs[i]
                e, w = free[q], last[q]
                for p, b in pre[i]:
                    x = end[p] + b
                    if x > e:
                        e, w = x, p
                e += cost[i] * slow[i]
                end[i], why[i], free[q], last[q] = e, w, e, i
                if e + tail[i] > top:
                    top, at = e + tail[i], i
            top += EARLY * sum(end) / n
            pairs = []
            while at >= 0:
                w = why[at]
                if w >= 0 and qs[w] == qs[at] and w not in before[at]:
                    pairs.append((w, at))
                at = w
            return top, pairs

        def flip(i):
            way[i] = 1 - way[i]
            q, _, c = nodes[i]["ways"][way[i]]
            qs[i], cost[i] = names.index(q), c
        seed = [SEED]

        def draw(m):
            seed[0] = (seed[0] * 1103515245 + 12345) % 2147483648
            return (seed[0] >> 8) % m
        now = [run(seq, f) for f in sets]
        total = sum(t for t, _ in now)
        best, kept = total, (seq, list(way))
        for step in range(TRIES):
            pairs = now[draw(len(sets))][1]
            room = SLACK * (1.0 - step / TRIES) * draw(1000) / 1000.0 * (draw(3) == 0)
            if draw(5) == 0:
                near = [x for p in pairs for x in p if nodes[x]["ways"][1]]
                i = near[draw(len(near))] if near and draw(2) else two[draw(len(two))]
                moved = [i]
                if draw(2):
                    b = seq.index(i)
                    near = [x for x in seq[max(0, b - 12):b + 12] if nodes[x]["ways"][1] and qs[x] != qs[i]]
                    if near:
                        moved.append(near[draw(len(near))])
                for x in moved:
                    flip(x)
                then = [run(seq, f) for f in sets]
                t = sum(x for x, _ in then)
                if t <= total + room:
                    now, total = then, t
                    if t < best:
                        best, kept = t, (seq, list(way))
                else:
                    for x in moved:
                        flip(x)
                continue
            if pairs and draw(4):
                j, i = pairs[draw(len(pairs))]
                a, b = seq.index(j), seq.index(i)
            else:
                b = 1 + draw(n - 1)
                i = seq[b]
                a = b - 1
                while a >= 0 and qs[seq[a]] != qs[i]:
                    a -= 1
                if a < 0:
                    continue
                j = seq[a]
            for _ in range(draw(3) if draw(2) else 0):
                a2 = a - 1
                while a2 >= 0 and qs[seq[a2]] != qs[i]:
                    a2 -= 1
                if a2 >= 0:
                    a = a2
            part = seq[a:b + 1]
            if draw(2):
                need = {part[-1]}
                for m in reversed(part[:-1]):
                    if any(m in before[x] for x in need):
                        need.add(m)
                if part[0] in need:
                    continue
                part = [m for m in part if m in need] + [m for m in part if m not in need]
            else:
                need = {part[0]}
                for m in part[1:]:
                    if before[m] & need:
                        need.add(m)
                if part[-1] in need:
                    continue
                part = [m for m in part if m not in need] + [m for m in part if m in need]
            other = seq[:a] + part + seq[b + 1:]
            then = [run(other, f) for f in sets]
            t = sum(x for x, _ in then)
            if t <= total + room:
                seq, now, total = other, then, t
                if t < best:
                    best, kept = t, (other, list(way))
        return kept

    def emit():
        count, free = {}, list(DMAS)
        known = {q: {} for q in queue}

        def need(q, s, n, more):
            if known[q].get(s, 0) < n:
                queue[q].wait_ge(T.sem[s], int(n))
                known[q][s] = n
            for s2, n2 in more.items():
                if known[q].get(s2, 0) < n2:
                    known[q][s2] = n2
        seq, way = order()
        for k, i in enumerate(seq):
            d = nodes[i]
            d["q"], d["call"], d["cost"] = d["ways"][way[i]]
            q, top = d["q"], {}
            for p in d["deps"]:
                o = nodes[p]
                if "s" in o and (o["s"] not in top or top[o["s"]]["n"] < o["n"]):
                    top[o["s"]] = o
            for o in sorted(top.values(), key=lambda o: -o["at"]):
                need(q, o["s"], o["n"], o["k"])
            ins = d["call"]()
            if d["kind"] in ("op", "dma"):
                if d["kind"] == "dma":
                    s, n, up = free.pop(0), 16, 16
                else:
                    s, up = sem_of[q], 1
                    n = count.get(s, 0) + 1
                ins.then_inc(T.sem[s], up)
                count[s] = n
                d["s"], d["n"], d["k"], d["at"] = s, n, dict(known[q]), k
        for s, n in count.items():
            need("g", s, n, {})
    return op, emit


def rank_program(g, core, T, topo):
    rank = T.rank_of(core)
    if rank is None:
        return
    op, emit = planner(g, T)
    M = AluOpType
    AF = ActivationFunctionType
    ts_, tt_ = g.vector.tensor_scalar, g.vector.tensor_tensor
    to, frm = T.cores[(rank - 1) % len(T.cores)], T.cores[(rank + 1) % len(T.cores)]
    CY = 0.83

    def ap(r):
        t = T[r[0]]
        return t[:, r[1]:r[2]:r[3]] if len(r) == 4 else t[:, r[1]:r[2]]

    def wide(r):
        return len(range(r[1], r[2], r[3] if len(r) == 4 else 1))

    def half(*rs):
        return 0.5 if all(SCRATCH[r[0]][2] == BF for r in rs) else 1.0

    def slot(r, i, step=4):
        return (r[0], r[1] + i, r[2], step)

    def cols(s):
        return [x for x in s if not isinstance(x, (int, float))]

    def val(s):
        return s if isinstance(s, (int, float)) else ap(s)

    used = [0]

    def new(n):
        n0 = used[0]
        used[0] = n0 + n + (-n) % 4
        return ("WK", n0, n0 + n)

    def ts(out, in0, s1, op0, s2=None, op1=None):
        out = out or new(wide(in0))
        if op1 is None:
            op("v", lambda: ts_(ap(out), ap(in0), val(s1), None, op0), [in0] + cols([s1]), [out], CY * max(64, wide(in0)))
        else:
            op("v", lambda: ts_(ap(out), ap(in0), val(s1), val(s2), op0, op1), [in0] + cols([s1, s2]), [out], CY * max(64, wide(in0)))
        return out

    def tt(out, in0, in1, o):
        out = out or new(wide(in0))
        op("v", lambda: tt_(ap(out), ap(in0), ap(in1), o), [in0, in1], [out], CY * max(64, wide(in0) * (1 if in0[0][0] == "P" else 2)))
        return out

    def scan(out, d0, d1, op0, op1, first=0.0):
        out = out or new(wide(d0))
        op("v", lambda: g.vector.tensor_tensor_scan(ap(out), ap(d0), ap(d1), first, op0, op1), [d0, d1], [out], CY * max(64, wide(d0)))
        return out

    def either(q, reads, out, on_v, on_s):
        ways = [("v",) + on_v, ("a",) + on_s]
        if q == "a":
            ways.reverse()
        op(ways[0][0], ways[0][1], reads, [out], ways[0][2], other=ways[1])
        return out

    def cp(out, in0, q=None):
        on_v = (lambda: g.vector.tensor_copy(ap(out), ap(in0)), CY * max(64, wide(in0) * half(out, in0)))
        if q is None:
            return op("v", on_v[0], [in0], [out], on_v[1])
        either(q, [in0], out, on_v, (lambda: g.scalar.activation(ap(out), ap(in0), AF.Copy), 20 + CY * max(64, wide(in0))))

    def fill(out, x, q=None):
        on_v = (lambda: g.vector.memset(ap(out), x), CY * max(64, wide(out) * half(out)))
        if q is None:
            return op("v", on_v[0], [], [out], on_v[1])
        src = ("low", 0, wide(out))
        either(q, [src], out, on_v, (lambda: g.scalar.activation(ap(out), ap(src), AF.Identity, bias=x, scale=0.0), 20 + CY * max(64, wide(out))))

    def lin(q, out, in0, scale, bias):
        out = out or new(wide(in0))
        return either(q, [in0] + cols([scale, bias]), out,
                      (lambda: ts_(ap(out), ap(in0), val(scale), val(bias), M.mult, M.add), CY * max(64, wide(in0) * half(out, in0))),
                      (lambda: g.scalar.activation(ap(out), ap(in0), AF.Identity, bias=val(bias), scale=val(scale)), 20 + CY * max(64, wide(in0))))

    def act(out, in0, func, bias=0.0, scale=1.0):
        out = out or new(wide(in0))
        op("a", lambda: g.scalar.activation(ap(out), ap(in0), func, bias=val(bias), scale=val(scale)), [in0] + cols([bias, scale]), [out],
           20 + CY * max(64, wide(in0)))
        return out

    def gather(q, out, win, off, scale=None):
        cost = 1.5 * CY * wide(out)
        if scale is not None:
            either(q, [win, off], out, (lambda: ts_(ap(out), ap(win).indirect(ap(off)), scale, None, M.mult), 50 + cost),
                   (lambda: g.scalar.activation(ap(out), ap(win).indirect(ap(off)), AF.Copy, scale=scale), 65 + cost))
        else:
            either(q, [win, off], out, (lambda: g.vector.tensor_copy(ap(out), ap(win).indirect(ap(off))), 50 + cost),
                   (lambda: g.scalar.activation(ap(out), ap(win).indirect(ap(off)), AF.Copy), 65 + cost))

    def quant(q, s, lo, n, tile):
        op("v", lambda: g.vector.quantize_mx(T[q][:, lo:lo + n], T[s][:, lo:lo + n], ap(tile)), [tile], [(q, lo, lo + n), (s, lo, lo + n)], 12 + 0.88 * n)

    def mm(bank, n, w, ws, wl, x, xs, xl, start=True, stop=True, after=None):
        out = ("P%d" % bank, 0, 512)
        return op("t", lambda: g.tensor.matmul_mx(T[out[0]][:, 0:n], T[w][:, wl:wl + 128], T[ws][:, wl:wl + 128], T[x][:, xl:xl + n], T[xs][:, xl:xl + n],
                                                  start, stop),
                  [(w, wl, wl + 128), (ws, wl, wl + 128), (x, xl, xl + n), (xs, xl, xl + n)], [out], 0.6 * (n + 16), acc=not start, after=after)

    dq, dmas = {"sy": g.sync, "a": g.scalar, "g": g}, {}

    def load(q, out, src):
        dst = ap(out).bitcast(dt.uint8) if out[0] == "WQ" else ap(out)
        dmas[q] = op(q, lambda: dq[q].dma_start(dst, src), [], [out], 60.0, "dma", late=LOAD, after=dmas.get(q))

    def store(q, dst, src, reg):
        op(q, lambda: dq[q].dma_start(dst, src), [reg], [], 60.0, "dma", late=LOAD)

    def iota(out, pattern, base, mult):
        cost = 130 + 2 * CY * wide(out)
        if SCRATCH[out[0]][2] == F32:
            op("g", lambda: g.iota(ap(out), pattern, base, mult, allow_small_or_imprecise_dtypes=True), [], [out], cost)
        else:
            op("g", lambda: g.iota(ap(out), pattern, base, mult), [], [out], cost)

    def x(lo, hi, lane=None):
        return ("X", PAD + 4 * lo, PAD + 4 * hi) if lane is None else ("X", PAD + 4 * lo + lane, PAD + 4 * hi, 4)

    load("sy", x(A, H), T.x[:, 4 * A:4 * H])
    load("a", ("ut", 0, 512), T.u[:, :])
    load("sy", x(H, C), T.x[:, 4 * H:4 * C])
    load("sy", x(0, A), T.x[:, 0:4 * A])
    load("sy", ("WQ", 0, 512), T.wc[:, :])
    load("sy", ("WS", 0, 512), T.ws[:, :])
    load("sy", ("vt", 0, 512), T.v[:, :])

    iota(("pi", 0, 1), [[1, 1]], 0, 1)
    iota(("KI", 0, 128), [[1, 128]], 0, -1)
    iota(("m16", 0, 28), [[16, 28]], 0, 0)
    iota(("ulist", 0, 16), [[1, 2], [16, 8]], 0, 0)
    iota(("mp", 0, 2 * NP), [[CUT, 2], [16, NP]], 0, 0)
    iota(("mj", 0, 2 * NC), [[0, 2], [16, NC]], 0, 0)
    low = ("low", 0, 96)
    fill(low, -1.0e29)
    fill(("EH", 0, 528), 0.0)
    ts(("EH", 3, 515, 4), ("KI", 0, 128), 0.0, M.is_equal, 0.5, M.mult)
    lin("a", ("EB", 0, 520), ("EH", 0, 520), 64.0, 0.0)
    ts(("pa", 0, 1), ("pi", 0, 1), 15, M.bitwise_and)
    pf = ("pf", 0, 1)
    cp(pf, ("pa", 0, 1))
    fill(("X", 0, PAD), 0.0)
    fill(("Bt", 4 * K, 512), 0.0)
    cp(("uoff", 0, 16), ("ulist", 0, 16))
    zs = ("ZS", 0, 336)
    SV, B0, N0, R0, R1 = ("ZS", 0, 4 * NS), ("ZS", 64, 100), ("ZS", 100, 100 + 4 * NJ), ("ZS", 192, 192 + 4 * NC), ("ZS", 264, 264 + 4 * NC)
    B1, W1, U1, U2, N1, PAT = ("B1", 0, 36), ("W1", 0, 4 * NA), ("U1", 0, 2 * NA), ("U2", 0, 2 * NA), ("N1", 0, 4 * NJ), ("PAT", 0, 4 * NA)
    fill(zs, 0.0)
    fill(PAT, 1.0, "v")
    fill(slot(PAT, 0), 0.0, "v")
    fill(slot(PAT, 1), -1.0, "v")
    ts(("ei", 0, 28), ("m16", 0, 28), pf, M.add)
    ts(("zi", 0, 12), ("ei", 16, 28), 2, M.arith_shift_right)
    ZQ, NZ, ET = ("ZQ", 0, 12), ("NZ", 0, 12), ("ET", 0, 16)
    ts(ZQ, ("zi", 0, 12), L2 + 0.5, M.add)
    ts(NZ, ("zi", 0, 12), -1.0, M.mult, float(C - L1 - L2), M.add)
    ts(slot(B1, 1, 3), ("zi", 0, 12), -2.0, M.mult, -1.0, M.add)
    ts(ET, ("ei", 0, 16), 0.25, M.mult, L1 - L2 + PAD / 4, M.add)
    ts(slot(B1, 2, 3), ("ei", 16, 28), 0.25, M.mult, L1 - L2 + PAD / 4, M.add)
    PL, PB, J, J2, J6 = ("PL", 0, NA), ("PB", 0, NA), ("J", 0, NJ), ("J2", 0, NJ), ("J6", 0, NJ)
    lin("a", PL, ("mp", 0, NA), 1.0, pf)
    lin("a", J, ("mj", 0, NJ), 1.0, pf)
    lin("a", PB, PL, -2048.0, 0.0)
    lin("a", slot(W1, 1), PL, -1.0, 0.0)
    fill(slot(U1, 0, 2), BIG, "a")
    fill(slot(U2, 0, 2), -BIG, "a")
    lin("a", J2, J, 0.5, 0.0)
    lin("a", J6, J, -1.0 / 6.0, 0.0)
    fill(slot(N0, 0), -BIG, "a")
    lin("a", slot(N0, 3), J, 0.5, -0.35)
    lin("a", slot(N1, 0), J, -0.25, 0.0)
    fill(slot(N1, 3), -BIG, "a")
    for t, f in (("CK", lambda e: e[2]), ("CC", lambda e: e[1])):
        fill((t, 0, NS), 0.0, "v")
        i = 0
        while i < NS:
            j = i
            while j < NS and f(SCAL[j]) == f(SCAL[i]):
                j += 1
            if f(SCAL[i]) != 0.0:
                fill((t, i, j), float(f(SCAL[i])), "v" if t == "CC" else "a")
            i = j
    for i, e in enumerate(SCAL):
        fill(("ZS", 4 * i, 4 * i + 1), -(e[3] + L1 * e[1] + L2 * e[2]), "a")

    quant("QU", "SU", 0, 128, ("ut", 0, 512))
    op("v", lambda: g.vector.tensor_copy(T.QUU[:, 0:256].bitcast(dt.uint32), T.QU[:, 0:128].bitcast(dt.uint32).indirect(T.uoff[:, 0:16])),
       [("QU", 0, 128), ("uoff", 0, 16)], [("QUU", 0, 256)], 380.0)
    op("a", lambda: g.scalar.activation(T.SUU[:, 0:256], T.SU[:, 0:128].indirect(T.uoff[:, 0:16]), AF.Copy), [("SU", 0, 128), ("uoff", 0, 16)],
       [("SUU", 0, 256)], 400.0)

    for r in range(ROUNDS):
        last = r == ROUNDS - 1
        qx, sx, qb, sb, lb, la, lx = ["%s%d" % (s, r) for s in ("QX", "SX", "QB", "SB", "lb", "la", "lx")]
        quant("QS", "SS", 0, 128, x(A, H))
        mm(4, 128, "QUU", "SUU", 0, "QS", "SS", 0, after=mm(5, 128, "QUU", "SUU", 128, "QS", "SS", 0))

        def first(bank, lo, n, after):
            m, out = new(n), new(1)
            run = scan(None, ("P%d" % bank, lo, lo + n), ("low", 0, n), M.max, M.max, -1.0e29)
            top = ("WK", run[2] - 1, run[2])
            return out, op("a", lambda: g.scalar.activation(ap(m), ap(run), AF.Sign, bias=ap(top), scale=-1.0, accum_out=ap(out)), [run], [m, out],
                           100.0, after=after)
        kk, i = first(5, L2 - A, H2 - L2 + 1, None)
        cc, i = first(4, L1 - A, H1 - L1 + 1, i)
        xs = ("X", 0, PAD + 4 * C)
        ts(slot(B1, 0, 3), ZQ, kk, M.add, 2.0, M.mult)
        ts(slot(B0, 2, 3), ZQ, -2.0 * L2 - 0.5, M.add, kk, M.is_ge)
        ts(slot(B0, 1, 3), NZ, cc, M.subtract, kk, M.is_gt)
        dd = lin("v", None, kk, -1.0, cc)
        bs = scan(None, B0, B1, M.mult, M.add)
        ts((lb, 0, 16), ET, dd, M.add, 4.0, M.mult)
        ts((lb, 16, 28), slot(bs, 2, 3), dd, M.add, 4.0, M.mult)
        gather("a", ("Bt", 0, 160), xs, (lb, 0, 10))
        gather("v", ("Bt", 160, 256), xs, (lb, 10, 16))
        gather("v", ("Bt", 256, 352), xs, (lb, 16, 22))
        gather("a", ("Bt", 352, 448), xs, (lb, 22, 28))
        quant(qb, sb, 0, 128, ("Bt", 0, 512))
        rid, pid = topo.addr(to, core)
        mask = topo.mask(core, to)

        def send(qx=qx, sx=sx, qb=qb, sb=sb, r=r):
            g.remote_dma(T[qx][:, C:C + K].bitcast(dt.uint8), T[qb][:, 0:K].bitcast(dt.uint8), T.sem["came%d" % r], T.sem.gone, pid, rid, mask)
            g.remote_dma(T[sx][:, C:C + K], T[sb][:, 0:K], T.sem["came%d" % r], T.sem.gone, pid, rid, mask)
        sent = op("g", send, [(qb, 0, 128), (sb, 0, 128)], [], 600.0, "send", late=EXCHANGE)
        if r == 0:
            for b in range(4):
                quant("QEH", "SEH", 128 * b, 128, ("EH", 3 - b, 515 - b))
        quant(qx, sx, 0, C, x(0, C))
        for b in range(4):
            mm(b, C, "QEH", "SEH", 128 * b, qx, sx, 0)
            cp(("FG", FW * b, FW * b + C), ("P%d" % b, 0, C), "a")
            cp(("FO", CUT * b, CUT * b + CUT), ("FG", FW * b, FW * b + CUT), "v")
        if r == 0:
            for b in range(4):
                quant("QEB", "SEB", 128 * b, 128, ("EB", 3 - b, 515 - b))
        for b in range(4):
            mm(4 + b, CUT, "QEB", "SEB", 128 * b, qx, sx, 0, True, False)
        lin("a", slot(SV, 2), ("CK", 0, NS), kk, 0.0)
        lin("a", slot(SV, 1), ("CC", 0, NS), cc, 0.0)
        sv = scan(None, ("PAT", 0, 4 * NS), SV, M.mult, M.add)
        sc = {e[0]: ("WK", sv[1] + 4 * i + 3, sv[1] + 4 * i + 4) for i, e in enumerate(SCAL)}
        ts(slot(W1, 0), PL, sc["s"], M.is_ge, sc["k2"], M.mult)
        ts(slot(W1, 3), PL, sc["cm"], M.is_ge, sc["k2"], M.mult)
        ts(slot(W1, 2), PB, sc["fb"], M.add, sc["c2"], M.max)
        a1 = act(None, PL, AF.Abs, bias=sc["cm"], scale=-1.0)
        w = scan(None, PAT, W1, M.mult, M.add)
        ts(slot(U1, 1, 2), slot(w, 3), 0.5, M.is_lt, 4096.0, M.mult)
        lin("a", slot(w, 1), PL, 1.0, sc["nalt"])
        w = scan(None, U1, slot(w, 1, 2), M.add, M.min)
        ts(slot(U2, 1, 2), slot(w, 1, 2), -287.5, M.is_ge, -4096.0, M.mult)
        act(slot(w, 0, 2), a1, AF.Abs, bias=sc["nk"])
        w = scan(None, U2, w, M.add, M.max)
        ts((la, 0, NA), slot(w, 1, 2), 287.5, M.add)
        j0 = 0 if last else A // 16
        n0, n1 = (N0[0], N0[1] + 4 * j0, N0[1] + 4 * (j0 + NC)), (N1[0], 4 * j0, 4 * (j0 + NC))
        o = sc["a1"][1]
        ln = tt(None, ("WK", o, o + 9, 4), ("WK", o + 12, o + 21, 4), M.max)
        ln = [("WK", ln[1] + i, ln[1] + i + 1) for i in range(3)]
        ts(slot(n1, 1), ("J6", j0, j0 + NC), ln[0], M.add, ln[1], M.max)
        lin("a", slot(n1, 2), ("J2", j0, j0 + NC), 1.0, ln[2])
        o = new(4 * NC + 4)
        hi = slot(scan((o[0], o[1], o[2] - 4), n0, n1, M.add, M.max), 3)
        o = (o[0], o[1] + 1, o[2] - 3)
        ts(slot(o, 0), hi, WHOLE, M.add, -WHOLE, M.add)
        ts(slot(R1, 0), hi, WHOLE, M.add, -WHOLE, M.add)
        ts(slot(o, 1), hi, sc["kh"], M.is_ge, 0.55, M.mult)
        ts(slot(o, 3), hi, sc["n2h"], M.is_ge, 0.17, M.mult)
        y = scan(None, ("PAT", 0, 4 * NC), o, M.mult, M.add)
        act(slot(R0, 1), slot(y, 2), AF.Sign, bias=-0.10)
        ts(slot(R1, 1), slot(y, 2), 0.10, M.is_ge, sc["kh"], M.add)
        act(slot(R0, 2), slot(y, 3), AF.Sign, bias=0.14)
        act(slot(R0, 3), slot(y, 3), AF.Sign, bias=0.35, scale=-1.0)
        y = scan(None, R0, R1, M.mult, M.add)
        ts((lx, 0, NC), slot(y, 3), sc["cm"], M.add)
        if last:
            iota(("CJ", 0, C), [[1, C]], 0, 0)
            quant("QV", "SV", 0, 128, ("vt", 0, 512))
            gather("a", ("LO", 0, C), ("CJ", 0, C), (lx, 0, NC))
        came = op("t", lambda r=r: g.tensor.wait_ge(T.sem["came%d" % r], 2 * len(topo.engines(frm, core))), [], [], 0.0, "wait", after=sent)
        n2 = C - CUT
        for b in range(4):
            mm(b, 128, "QEH", "SEH", 128 * b, qx, sx, C + K - 128, after=came)
        for b in range(4):
            cp(("FG", FW * b + C, FW * b + FW), ("P%d" % b, 128 - K, 128), "av"[b % 2])
        for b in range(4):
            mm(b, n2, "QEB", "SEB", 128 * b, qx, sx, CUT, True, False)
        for b in range(4):
            win = ("FG", FW * b, FW * b + FW)
            gather("a", ("AN", n2 * b, n2 * b + n2), win, (la, NP, NA))
            off, own, out = (la, 0, CUT // 16), ("FO", CUT * b, CUT * b + CUT), ("Z", b, 4 * CUT, 4)
            op("v", lambda win=win, off=off, own=own, out=out: tt_(ap(out), ap(win).indirect(ap(off)), ap(own), M.add), [win, off, own], [out], 50 + 1.5 * CY * CUT)
        quant("QZ", "SZ", 0, CUT, ("Z", 0, 4 * CUT))
        for b in range(4):
            mm(4 + b, CUT, "WQ", "WS", 128 * b, "QZ", "SZ", 0, False, True)
        for b in range(4):
            tt(("Z", 4 * CUT + b, 4 * C, 4), ("P%d" % b, CUT, C), ("AN", n2 * b, n2 * b + n2), M.add)
        quant("QZ", "SZ", CUT, n2, ("Z", 4 * CUT, 4 * C))
        for b in range(4):
            mm(b, n2, "WQ", "WS", 128 * b, "QZ", "SZ", CUT, False, True)
        for b in range(4):
            cp(("Y", C * b, C * b + CUT), ("P%d" % (4 + b), 0, CUT), "a")
        for b in range(4):
            cp(("Y", C * b + CUT, C * b + C), ("P%d" % b, 0, n2), "va"[b % 2])
        if not last:
            for b in range(4):
                gather("va"[b % 2], x(A, H, b), ("Y", C * b, C * b + C), (lx, 0, (H - A) // 16), 0.03125)
            for b in range(4):
                gather("vaaa"[b], x(H, C + A, b), ("Y", C * b, C * b + C), (lx, (H - A) // 16, NC), 0.03125)
            cp(x(0, A), x(C, C + A), "v")
            continue
        for b in range(4):
            gather("va"[b % 2], x(0, C, b), ("Y", C * b, C * b + C), (lx, 0, NC), 0.03125)
        cut = 144
        for i, (lo, hi) in enumerate(((0, cut), (cut, C))):
            quant("QL", "SL", lo, hi - lo, x(lo, hi))
            mm(4 + i, hi - lo, "QV", "SV", 0, "QL", "SL", lo)
        cp(("yt", 0, cut), ("P4", 0, cut), "v")
        cp(("yt", cut, C), ("P5", 0, C - cut), "v")
        store("sy", T.oc[:, :], T.QL[:, 0:C].bitcast(dt.uint8), ("QL", 0, C))
        for k in range(4):
            store("a", T.osc[4 * k:4 * k + 4, 0:C], T.SL[32 * k:32 * k + 4, 0:C], ("SL", 0, C))
        store("sy", T.y[:, :], T.yt[:, 0:C], ("yt", 0, C))
        store("a", T.lo[:, :], T.LO[0:128:16, :], ("LO", 0, C))
    emit()
    g.wait_ge(T.sem.gone, 2 * ROUNDS * len(topo.engines(core, to)))
